import numpy as np
import ml_dtypes


def mxq(x, axis, fmt="e4m3"):
    dtype, down = {"e4m3": (ml_dtypes.float8_e4m3fn, 7), "e5m2": (ml_dtypes.float8_e5m2, 14)}[fmt]
    v = np.moveaxis(np.asarray(x, np.float32).astype(ml_dtypes.bfloat16).astype(np.float64), axis, -1)
    blocks = v.reshape(v.shape[:-1] + (-1, 32))
    amax = np.abs(blocks).max(-1, keepdims=True)
    byte = np.maximum(np.where(amax > 0, np.frexp(amax)[1] - 1 + 127, 0) - down, 1)
    scale = np.exp2(byte - 127.0)
    codes = (blocks / scale).astype(np.float32).astype(dtype).astype(np.float64)
    return np.moveaxis((codes * scale).reshape(v.shape), -1, axis)


WIDE = False


def mx_kscale(k):
    if not WIDE:
        return np.ones(k)
    levels = np.array([10, -10, 5, -5, 0])
    if k % 512:
        return np.exp2(np.random.permutation(np.resize(levels, k // 32))).repeat(32)
    a = np.empty((k // 512, 16))
    for p in range(k // 512):
        a[p, :8] = np.random.permutation(np.resize(levels, 8))
        for g in range(8):
            far = levels[np.abs(levels - a[p, g]) >= 10]
            a[p, g + 8] = far[np.random.randint(len(far))]
    return np.exp2(a.ravel()).repeat(32)


def f64(x):
    return np.asarray(x).astype(np.float64)


def striped(idx):
    return np.tile(idx.reshape(-1, 16).T, (8, 1)).astype(np.uint16)


def unstriped(offs):
    return offs[:16].T.reshape(-1).astype(np.int64)


E2M1 = np.array([0.0, 0.5, 1.0, 1.5, 2.0, 3.0, 4.0, 6.0, -0.0, -0.5, -1.0, -1.5, -2.0, -3.0, -4.0, -6.0])


def pack_weight(w, fmt):
    k, n = w.shape
    w = f64(np.asarray(w, np.float32).astype(ml_dtypes.bfloat16)).reshape(k // 32, 32, n)
    amax = np.abs(w).max(1)
    if fmt == "e4m3":
        byte = np.frexp(amax)[1] - 1 + 127 - 7
    else:
        mant, ex = np.frexp(amax / 6.0)
        byte = np.where(mant > 0.5, ex, ex - 1) + 127
    byte = np.clip(np.where(amax > 0, byte, 1), 1, 254)
    scaled = (w * np.exp2(127.0 - byte)[:, None, :]).reshape(k, n).astype(np.float32)
    by_word = np.ascontiguousarray(scaled.reshape(k // 512, 128, 4, n).transpose(0, 1, 3, 2))
    if fmt == "e4m3":
        words = by_word.astype(ml_dtypes.float8_e4m3fn).view(np.uint8)
    else:
        c = by_word.astype(ml_dtypes.float4_e2m1fn).view(np.uint8) & 0xF
        words = (c[..., 0::2] | (c[..., 1::2] << 4)).reshape(k // 512, 128, 2 * n)
    return np.ascontiguousarray(words), np.ascontiguousarray(byte.astype(np.uint8).reshape(k // 512, 16, n))


def unpack_weight(words, scales, fmt):
    g, _, n = scales.shape
    words = np.ascontiguousarray(words).reshape(g, 128, n, -1)
    if fmt == "e4m3":
        vals = words.view(ml_dtypes.float8_e4m3fn).astype(np.float64)
    else:
        nib = np.empty((g, 128, n, 4), np.uint8)
        nib[..., 0::2] = words & 0xF
        nib[..., 1::2] = words >> 4
        vals = E2M1[nib]
    vals = vals * np.repeat(np.exp2(scales.astype(np.float64) - 127.0), 8, axis=1)[..., None]
    return vals.transpose(0, 1, 3, 2).reshape(g * 512, n)


def d_relu2(v):
    return 2.0 * np.maximum(v, 0.0)


K, T, E, C, H, N = 512, 512, 8, 128, 512, 512


def by_expert(wq, xq):
    return np.concatenate([wq[e].T @ xq[:, e * C:(e + 1) * C] for e in range(E)], axis=1)


def setup_inputs():
    n = np.random.standard_normal
    v = mx_kscale(N)
    u = mx_kscale(H)
    first = np.random.permutation(np.repeat(np.arange(E), T // E))
    second = (first + 1 + np.random.permutation(np.repeat(np.arange(E - 1), -(-T // (E - 1)))[:T])) % E
    while np.bincount(second, minlength=E).max() != T // E:
        load = np.bincount(second, minlength=E); hi, lo = int(load.argmax()), int(load.argmin())
        t = np.flatnonzero((second == hi) & (first != lo))[0]; second[t] = lo
    slot_token = np.empty(E * C, np.int64); pos = np.empty((2, T), np.int64); fill = np.zeros(E, np.int64)
    place = np.stack([np.random.permutation(C) for _ in range(E)])
    for r, deal in enumerate((first, second)):
        for t in np.random.permutation(T):
            e = deal[t]; j = e * C + place[e, fill[e]]; fill[e] += 1; slot_token[j] = t; pos[r, t] = j
    g = np.random.uniform(0.2, 0.8, T)
    w_slot = np.empty(E * C); w_slot[pos[0]] = g; w_slot[pos[1]] = 1.0 - g
    dy = pack_weight(n((N, T)) * v[:, None], "e4m3")
    w2t = pack_weight(n((N, H)) / np.sqrt(N) / v[:, None] * u, "e2m1")
    w1t = [pack_weight(m, "e2m1") for m in n((E, H, K)) / np.sqrt(H) / u[None, :, None]]
    return {
        "dy_words": dy[0],
        "dy_scales": dy[1],
        "w2t_words": w2t[0],
        "w2t_scales": w2t[1],
        "w1t_words": np.stack([m[0] for m in w1t]),
        "w1t_scales": np.stack([m[1] for m in w1t]),
        "a": (n((H, E * C))).astype(np.float32),
        "gate": (np.tile(w_slot, (128, 1))).astype(np.float32),
        "offs": striped(slot_token),
        "pos1": striped(pos[0]),
        "pos2": striped(pos[1]),
    }


def reference(dy_words, dy_scales, w2t_words, w2t_scales, w1t_words, w1t_scales, a, gate, offs, pos1, pos2):
    w2t = unpack_weight(w2t_words, w2t_scales, "e2m1")
    w1t = np.stack([unpack_weight(w1t_words[e], w1t_scales[e], "e2m1") for e in range(E)])
    idx = unstriped(offs)
    dc = w2t.T @ unpack_weight(dy_words, dy_scales, "e4m3")
    da = f64(gate[:1]) * dc[:, idx] * d_relu2(f64(a))
    dx = by_expert(w1t, mxq(da, 0, "e4m3"))
    out = dx[:, unstriped(pos1)] + dx[:, unstriped(pos2)]
    return out

@@ -1,0 +1,177 @@
+from contextlib import ExitStack
+
+import concourse.mybir as mybir
+from concourse.masks import make_identity
+
+K, T, E, C, H, N = 512, 512, 8, 128, 512, 512
+S = E * C
+P = 128
+FLOPS = 2 * N * H * T + 2 * H * K * S
+
+F32 = mybir.dt.float32
+BF16 = mybir.dt.bfloat16
+I32 = mybir.dt.int32
+U32 = mybir.dt.uint32
+U16 = mybir.dt.uint16
+U8 = mybir.dt.uint8
+FP8X4 = mybir.dt.float8_e4m3fn_x4
+FP4X4 = mybir.dt.float4_e2m1fn_x4
+MULT = mybir.AluOpType.mult
+ADD = mybir.AluOpType.add
+COPY = mybir.ActivationFunctionType.Copy
+RELU = mybir.ActivationFunctionType.Relu
+
+GROUPS = [(0, 2), (2, 2), (4, 2), (6, 1), (7, 1)]
+RELU_ON_SCALAR = (2,)
+BANKS0 = [(0, 4), (4, 3), (7, 1)]
+BANKS = [(0, 4), (4, 4)]
+TAIL = [(0, 256), (256, 128), (384, 128)]
+
+
+def tile_moe_sdb_relu2_kernel(
+    tc, dy_words, dy_scales, w2t_words, w2t_scales, w1t_words, w1t_scales, a, gate, offs, pos1, pos2, out
+):
+    nc = tc.nc
+    with ExitStack() as ctx:
+        keep = ctx.enter_context(tc.tile_pool(name="keep", bufs=1))
+        ring = ctx.enter_context(tc.tile_pool(name="ring", bufs=2))
+        ps_mm = ctx.enter_context(tc.psum_pool(name="ps_mm", bufs=4))
+        ps_tr = ctx.enter_context(tc.psum_pool(name="ps_tr", bufs=2))
+
+        offs_t = keep.tile([P, S // 16], U16, name="offs_t")
+        pos1_t = keep.tile([P, T // 16], U16, name="pos1_t")
+        pos2_t = keep.tile([P, T // 16], U16, name="pos2_t")
+        dy_w = keep.tile([P, T], U32, name="dy_w", align_bytes=64)
+        head_s = keep.tile([P, T + H], U8, name="head_s", align_bytes=64)
+        dy_s = head_s[:, 0:T]
+        w2_w = keep.tile([P, 2 * H], U8, name="w2_w", align_bytes=64)
+        w1_w = keep.tile([P, E, 2 * K], U8, name="w1_w", align_bytes=64)
+        w1_s = keep.tile([P, E, K], U8, name="w1_s", align_bytes=64)
+        ident = keep.tile([P, P], F32, name="ident")
+        gate_rows = keep.tile([P, C], F32, name="gate_rows")
+        gate2 = keep.tile([P, E], F32, name="gate2")
+
+        nc.gpsimd.memset(head_s[:].bitcast(I32), 0)
+        nc.vector.memset(gate_rows[:], 0.0)
+        nc.vector.memset(w1_s[:].rearrange("p e k -> p (e k)").bitcast(I32), 0)
+        make_identity(nc, ident[:])
+
+        nc.sync.dma_start(dy_w[:].bitcast(I32), dy_words[0].rearrange("p t d -> p (t d)").bitcast(I32))
+        nc.sync.dma_start(w2_w[:].bitcast(I32), w2t_words[0].bitcast(I32))
+        for r in range(4):
+            nc.sync.dma_start(head_s[r:P:32, T : T + H].bitcast(I32), w2t_scales[0, r:16:4, :].bitcast(I32))
+        for r in range(4):
+            queue = nc.sync
+            queue.dma_start(head_s[r:P:32, 0:T].bitcast(I32), dy_scales[0, r:16:4, :].bitcast(I32))
+        nc.sync.dma_start(offs_t[:], offs)
+        a_planes = a.rearrange("(b p) s -> p b s", p=P)
+        a_t = []
+        for gi, (e0, n) in enumerate(GROUPS):
+            tile = keep.tile([P, 4, n * C], F32, name="a_%d" % gi)
+            nc.sync.dma_start(tile[:], a_planes[:, :, e0 * C : (e0 + n) * C])
+            a_t.append(tile)
+            if gi == 0:
+                nc.sync.dma_start(gate_rows[0:E, :], gate[0].rearrange("(e u) -> e u", u=C))
+        nc.sync.dma_start(w1_w[:].bitcast(I32), w1t_words.rearrange("e o p n -> p (e o) n").bitcast(I32))
+        for r in range(4):
+            nc.sync.dma_start(
+                w1_s[r:P:32, :, :].bitcast(I32),
+                w1t_scales[:, 0, r:16:4, :].rearrange("e q k -> q e k").bitcast(I32),
+            )
+        nc.sync.dma_start(pos1_t[:], pos1)
+        nc.sync.dma_start(pos2_t[:], pos2)
+
+        dc = []
+        for b in range(4):
+            acc = ps_mm.tile([P, T], F32, name="acc", tag="acc")
+            nc.tensor.matmul_mx(
+                out=acc[:],
+                lhsT=w2_w[:, 2 * P * b : 2 * P * (b + 1)].bitcast(FP4X4),
+                lhsT_scale=head_s[:, T + P * b : T + P * (b + 1)],
+                rhs=dy_w[:].bitcast(FP8X4),
+                rhs_scale=dy_s,
+                start=True,
+                stop=True,
+            )
+            plane = keep.tile([P, T], F32, name="dc_%d" % b)
+            nc.scalar.activation(plane[:], acc[:], COPY)
+            dc.append(plane)
+
+        gate_ps = ps_tr.tile([P, P], F32, name="gate_ps", tag="back")
+        nc.tensor.transpose(gate_ps[:], gate_rows[:], ident[:])
+        nc.scalar.activation(gate2[:], gate_ps[:, 0:E], COPY, scale=2.0)
+
+        codes = [keep.tile([P, C], U32, name="codes_%d" % e, align_bytes=64) for e in range(E)]
+        scales = [keep.tile([P, C], U8, name="scales_%d" % e, align_bytes=64) for e in range(E)]
+        dx = [keep.tile([P, S], F32, name="dx_%d" % b) for b in range(4)]
+
+        def products(b, e0, n):
+            acc = ps_mm.tile([P, T], F32, name="acc", tag="acc")
+            for e in range(e0, e0 + n):
+                nc.tensor.matmul_mx(
+                    out=acc[:, (e - e0) * C : (e - e0 + 1) * C],
+                    lhsT=w1_w[:, e, 2 * P * b : 2 * P * (b + 1)].bitcast(FP4X4),
+                    lhsT_scale=w1_s[:, e, P * b : P * (b + 1)],
+                    rhs=codes[e][:].bitcast(FP8X4),
+                    rhs_scale=scales[e][:],
+                    start=True,
+                    stop=True,
+                )
+            nc.scalar.activation(dx[b][:, e0 * C : (e0 + n) * C], acc[:, 0 : n * C], COPY)
+
+        for gi, (e0, n) in enumerate(GROUPS):
+            pos = keep.tile([P, 4, n * C], F32, name="pos_%d" % gi)
+            if gi in RELU_ON_SCALAR:
+                nc.scalar.activation(pos[:], a_t[gi][:], RELU)
+            else:
+                nc.vector.tensor_scalar_max(pos[:], a_t[gi][:], 0.0)
+            prod = ring.tile([P, 4, n * C], F32, name="prod", tag="prod")
+            window = offs_t[:, e0 * C // 16 : (e0 + n) * C // 16]
+            for b in range(4):
+                nc.vector.tensor_tensor(prod[:, b, :], dc[b][:].indirect(window), pos[:, b, :], MULT)
+            for e in range(e0, e0 + n):
+                turned = ps_tr.tile([P, H], F32, name="turned", tag="turned")
+                for b in range(4):
+                    nc.tensor.transpose(
+                        turned[:, b * P : (b + 1) * P], prod[:, b, (e - e0) * C : (e - e0 + 1) * C], ident[:]
+                    )
+                da_rows = ring.tile([P, 2, P, 2], BF16, name="da_rows", tag="da_rows")
+                nc.scalar.activation(
+                    da_rows[:],
+                    turned[:].rearrange("s (p u d) -> s u p d", u=2, d=2),
+                    COPY,
+                    scale=gate2[:, e : e + 1],
+                )
+                words = da_rows[:].rearrange("s u p d -> s (u p d)").bitcast(F32)
+                back = ps_tr.tile([P, 2, C], F32, name="back", tag="back")
+                for u in range(2):
+                    nc.tensor.transpose(back[:, u, :], words[:, u * P : (u + 1) * P], ident[:])
+                da = ring.tile([P, 4 * C], BF16, name="da", tag="da", align_bytes=64, bufs=8)
+                nc.scalar.copy(
+                    da[:].bitcast(F32).rearrange("p (s u) -> p s u", u=2), back[:].rearrange("p u s -> p s u")
+                )
+                nc.vector.quantize_mx(out=codes[e][:].bitcast(FP8X4), scales=scales[e][:], in_=da[:])
+
+        for e0, n in BANKS0:
+            products(0, e0, n)
+        for b in range(1, 4):
+            for e0, n in BANKS:
+                products(b, e0, n)
+
+        for b in range(4):
+            pieces = TAIL if b == 3 else [(0, 256), (256, 256)]
+            first = keep.tile([P, T], F32, name="first_%d" % b)
+            for t0, w in pieces:
+                nc.vector.tensor_copy(first[:, t0 : t0 + w], dx[b][:].indirect(pos1_t[:, t0 // 16 : (t0 + w) // 16]))
+            total = keep.tile([P, T], F32, name="total_%d" % b)
+            for t0, w in pieces:
+                nc.vector.tensor_tensor(
+                    total[:, t0 : t0 + w],
+                    dx[b][:].indirect(pos2_t[:, t0 // 16 : (t0 + w) // 16]),
+                    first[:, t0 : t0 + w],
+                    ADD,
+                )
+                if b == 3:
+                    nc.sync.dma_start(out[b * P : (b + 1) * P, t0 : t0 + w], total[:, t0 : t0 + w])
+            if b < 3:
+                nc.sync.dma_start(out[b * P : (b + 1) * P, :], total[:])

@@ -18,11 +18,12 @@ FP8X4 = mybir.dt.float8_e4m3fn_x4
 FP4X4 = mybir.dt.float4_e2m1fn_x4
 MULT = mybir.AluOpType.mult
 ADD = mybir.AluOpType.add
+MAX = mybir.AluOpType.max
 COPY = mybir.ActivationFunctionType.Copy
 RELU = mybir.ActivationFunctionType.Relu
 
-GROUPS = [(0, 2), (2, 2), (4, 2), (6, 1), (7, 1)]
-RELU_ON_SCALAR = (2,)
+DIRECT = 5
+A_LOADS = [(0, 2), (2, 2), (4, 1), (5, 2), (7, 1)]
 BANKS0 = [(0, 4), (4, 3), (7, 1)]
 BANKS = [(0, 4), (4, 4)]
 TAIL = [(0, 256), (256, 128), (384, 128)]
@@ -35,43 +36,59 @@ def tile_moe_sdb_relu2_kernel(
     with ExitStack() as ctx:
         keep = ctx.enter_context(tc.tile_pool(name="keep", bufs=1))
         ring = ctx.enter_context(tc.tile_pool(name="ring", bufs=2))
-        ps_mm = ctx.enter_context(tc.psum_pool(name="ps_mm", bufs=4))
-        ps_tr = ctx.enter_context(tc.psum_pool(name="ps_tr", bufs=2))
+        psum = ctx.enter_context(tc.psum_pool(name="psum", bufs=1))
+
+        def bank(number, shape):
+            return psum.tile(shape, F32, name="bank_%d" % number, tag="bank_%d" % number)
 
         offs_t = keep.tile([P, S // 16], U16, name="offs_t")
         pos1_t = keep.tile([P, T // 16], U16, name="pos1_t")
         pos2_t = keep.tile([P, T // 16], U16, name="pos2_t")
         dy_w = keep.tile([P, T], U32, name="dy_w", align_bytes=64)
         head_s = keep.tile([P, T + H], U8, name="head_s", align_bytes=64)
-        dy_s = head_s[:, 0:T]
+        w2_raw = keep.tile([P, 2 * H], U8, name="w2_raw", align_bytes=64)
         w2_w = keep.tile([P, 2 * H], U8, name="w2_w", align_bytes=64)
+        w2_s = keep.tile([P, H], U8, name="w2_s", align_bytes=64)
         w1_w = keep.tile([P, E, 2 * K], U8, name="w1_w", align_bytes=64)
         w1_s = keep.tile([P, E, K], U8, name="w1_s", align_bytes=64)
         ident = keep.tile([P, P], F32, name="ident")
         gate_rows = keep.tile([P, C], F32, name="gate_rows")
         gate2 = keep.tile([P, E], F32, name="gate2")
+        direct = 2 * C
+        gate_cols = keep.tile([P, direct], F32, name="gate_cols")
 
         nc.gpsimd.memset(head_s[:].bitcast(I32), 0)
         nc.vector.memset(gate_rows[:], 0.0)
         nc.vector.memset(w1_s[:].rearrange("p e k -> p (e k)").bitcast(I32), 0)
         make_identity(nc, ident[:])
 
+        a_planes = a.rearrange("(p t) s -> p t s", t=4)
+        a_tiles = [keep.tile([P, 4, n * C], F32, name="a_%d" % e0) for e0, n in A_LOADS]
+
+        def load_a(g):
+            e0, n = A_LOADS[g]
+            nc.sync.dma_start(a_tiles[g][:], a_planes[:, :, e0 * C : (e0 + n) * C])
+
+        def a_of(e, n):
+            g = max(i for i, (e0, count) in enumerate(A_LOADS) if e0 <= e)
+            j = e - A_LOADS[g][0]
+            return a_tiles[g][:, :, j * C : (j + n) * C]
+
+        nc.sync.dma_start(w2_raw[:].bitcast(I32), w2t_words[0].bitcast(I32))
         nc.sync.dma_start(dy_w[:].bitcast(I32), dy_words[0].rearrange("p t d -> p (t d)").bitcast(I32))
-        nc.sync.dma_start(w2_w[:].bitcast(I32), w2t_words[0].bitcast(I32))
         for r in range(4):
             nc.sync.dma_start(head_s[r:P:32, T : T + H].bitcast(I32), w2t_scales[0, r:16:4, :].bitcast(I32))
+        nc.sync.dma_start(gate_cols[:], gate[:, DIRECT * C : (DIRECT + 2) * C])
+        load_a(3)
         for r in range(4):
-            queue = nc.sync
-            queue.dma_start(head_s[r:P:32, 0:T].bitcast(I32), dy_scales[0, r:16:4, :].bitcast(I32))
+            nc.sync.dma_start(head_s[r:P:32, 0:T].bitcast(I32), dy_scales[0, r:16:4, :].bitcast(I32))
         nc.sync.dma_start(offs_t[:], offs)
-        a_planes = a.rearrange("(b p) s -> p b s", p=P)
-        a_t = []
-        for gi, (e0, n) in enumerate(GROUPS):
-            tile = keep.tile([P, 4, n * C], F32, name="a_%d" % gi)
-            nc.sync.dma_start(tile[:], a_planes[:, :, e0 * C : (e0 + n) * C])
-            a_t.append(tile)
-            if gi == 0:
-                nc.sync.dma_start(gate_rows[0:E, :], gate[0].rearrange("(e u) -> e u", u=C))
+        for h in range(0, 4, 2):
+            nc.sync.dma_start(a_tiles[0][:, h : h + 2, :], a_planes[:, h : h + 2, 0 : 2 * C])
+        load_a(1)
+        nc.sync.dma_start(gate_rows[0:E, :], gate[0].rearrange("(e u) -> e u", u=C))
+        load_a(4)
+        load_a(2)
         nc.sync.dma_start(w1_w[:].bitcast(I32), w1t_words.rearrange("e o p n -> p (e o) n").bitcast(I32))
         for r in range(4):
             nc.sync.dma_start(
@@ -81,32 +98,43 @@ def tile_moe_sdb_relu2_kernel(
         nc.sync.dma_start(pos1_t[:], pos1)
         nc.sync.dma_start(pos2_t[:], pos2)
 
+        nc.vector.tensor_copy(
+            w2_w[:].bitcast(U16).rearrange("p (t m) -> p t m", t=4),
+            w2_raw[:].bitcast(U16).rearrange("p (m t) -> p t m", t=4),
+        )
+        nc.vector.tensor_copy(
+            w2_s[:].rearrange("p (t m) -> p t m", t=4),
+            head_s[:, T : T + H].rearrange("p (m t) -> p t m", t=4),
+        )
+
         dc = []
-        for b in range(4):
-            acc = ps_mm.tile([P, T], F32, name="acc", tag="acc")
-            nc.tensor.matmul_mx(
-                out=acc[:],
-                lhsT=w2_w[:, 2 * P * b : 2 * P * (b + 1)].bitcast(FP4X4),
-                lhsT_scale=head_s[:, T + P * b : T + P * (b + 1)],
-                rhs=dy_w[:].bitcast(FP8X4),
-                rhs_scale=dy_s,
-                start=True,
-                stop=True,
-            )
-            plane = keep.tile([P, T], F32, name="dc_%d" % b)
-            nc.scalar.activation(plane[:], acc[:], COPY)
+        for t in range(4):
+            plane = keep.tile([P, T], F32, name="dc_%d" % t)
+            for n0, w in [(0, T // 2), (T // 2, T // 2)] if t == 0 else [(0, T)]:
+                acc = bank(4 if n0 else t, [P, T])
+                nc.tensor.matmul_mx(
+                    out=acc[:, 0:w],
+                    lhsT=w2_w[:, 2 * P * t : 2 * P * (t + 1)].bitcast(FP4X4),
+                    lhsT_scale=w2_s[:, P * t : P * (t + 1)],
+                    rhs=dy_w[:, n0 : n0 + w].bitcast(FP8X4),
+                    rhs_scale=head_s[:, n0 : n0 + w],
+                    start=True,
+                    stop=True,
+                )
+                nc.scalar.activation(plane[:, n0 : n0 + w], acc[:, 0:w], COPY)
             dc.append(plane)
 
-        gate_ps = ps_tr.tile([P, P], F32, name="gate_ps", tag="back")
+        gate_ps = bank(7, [P, P])
         nc.tensor.transpose(gate_ps[:], gate_rows[:], ident[:])
         nc.scalar.activation(gate2[:], gate_ps[:, 0:E], COPY, scale=2.0)
 
         codes = [keep.tile([P, C], U32, name="codes_%d" % e, align_bytes=64) for e in range(E)]
         scales = [keep.tile([P, C], U8, name="scales_%d" % e, align_bytes=64) for e in range(E)]
+        da = [keep.tile([P, 4 * C], BF16, name="da_%d" % e, tag="da_%d" % e, align_bytes=64) for e in range(E)]
         dx = [keep.tile([P, S], F32, name="dx_%d" % b) for b in range(4)]
 
-        def products(b, e0, n):
-            acc = ps_mm.tile([P, T], F32, name="acc", tag="acc")
+        def products(b, e0, n, evac, number):
+            acc = bank(number, [P, T])
             for e in range(e0, e0 + n):
                 nc.tensor.matmul_mx(
                     out=acc[:, (e - e0) * C : (e - e0 + 1) * C],
@@ -117,61 +145,104 @@ def tile_moe_sdb_relu2_kernel(
                     start=True,
                     stop=True,
                 )
-            nc.scalar.activation(dx[b][:, e0 * C : (e0 + n) * C], acc[:, 0 : n * C], COPY)
+            evac(dx[b][:, e0 * C : (e0 + n) * C], acc[:, 0 : n * C])
 
-        for gi, (e0, n) in enumerate(GROUPS):
-            pos = keep.tile([P, 4, n * C], F32, name="pos_%d" % gi)
-            if gi in RELU_ON_SCALAR:
-                nc.scalar.activation(pos[:], a_t[gi][:], RELU)
-            else:
-                nc.vector.tensor_scalar_max(pos[:], a_t[gi][:], 0.0)
-            prod = ring.tile([P, 4, n * C], F32, name="prod", tag="prod")
-            window = offs_t[:, e0 * C // 16 : (e0 + n) * C // 16]
-            for b in range(4):
-                nc.vector.tensor_tensor(prod[:, b, :], dc[b][:].indirect(window), pos[:, b, :], MULT)
+        def gathers(prod, factor, s0, w):
+            for t in range(4):
+                nc.vector.tensor_tensor(
+                    prod[:, t, :], dc[t][:].indirect(offs_t[:, s0 // 16 : (s0 + w) // 16]), factor[t], MULT
+                )
+
+        def quantize(e):
+            nc.vector.quantize_mx(out=codes[e][:].bitcast(FP8X4), scales=scales[e][:], in_=da[e][:])
+
+        gated = {}
+        for e0, n in [(5, 2)]:
+            tile = keep.tile([P, 4, n * C], F32, name="gated_%d" % e0)
+            cols = gate_cols[:, (e0 - DIRECT) * C : (e0 - DIRECT + n) * C]
+            nc.vector.scalar_tensor_tensor(
+                tile[:], a_of(e0, n), 0.0, cols.unsqueeze(1).broadcast_to([P, 4, n * C]), MAX, MULT
+            )
             for e in range(e0, e0 + n):
-                turned = ps_tr.tile([P, H], F32, name="turned", tag="turned")
-                for b in range(4):
-                    nc.tensor.transpose(
-                        turned[:, b * P : (b + 1) * P], prod[:, b, (e - e0) * C : (e - e0 + 1) * C], ident[:]
-                    )
+                gated[e] = [tile[:, t, (e - e0) * C : (e - e0 + 1) * C] for t in range(4)]
+
+        for e0, n in [(0, 2), (2, 2), (4, 1), (7, 1)]:
+            pos = keep.tile([P, 4, n * C], F32, name="pos_%d" % e0)
+            for h, w in [(0, 2), (2, 2)] if n == 2 else [(0, 4)]:
+                if e0 in (0,):
+                    nc.vector.tensor_scalar_max(pos[:, h : h + w, :], a_of(e0, n)[:, h : h + w, :], 0.0)
+                else:
+                    nc.scalar.activation(pos[:, h : h + w, :], a_of(e0, n)[:, h : h + w, :], RELU)
+            prod = ring.tile([P, 4, n * C], F32, name="prod", tag="prod")
+            gathers(prod, [pos[:, t, :] for t in range(4)], e0 * C, n * C)
+            for e in range(e0, e0 + n):
+                j = e - e0
+                turned = bank(4 + e % 2, [P, H])
+                for t in range(4):
+                    nc.tensor.transpose(turned[:, t * P : (t + 1) * P], prod[:, t, j * C : (j + 1) * C], ident[:])
                 da_rows = ring.tile([P, 2, P, 2], BF16, name="da_rows", tag="da_rows")
                 nc.scalar.activation(
                     da_rows[:],
-                    turned[:].rearrange("s (p u d) -> s u p d", u=2, d=2),
+                    turned[:].rearrange("s (u d p) -> s u p d", u=2, d=2),
                     COPY,
                     scale=gate2[:, e : e + 1],
                 )
                 words = da_rows[:].rearrange("s u p d -> s (u p d)").bitcast(F32)
-                back = ps_tr.tile([P, 2, C], F32, name="back", tag="back")
+                back = bank(6 + e % 2, [P, 2, C])
                 for u in range(2):
                     nc.tensor.transpose(back[:, u, :], words[:, u * P : (u + 1) * P], ident[:])
-                da = ring.tile([P, 4 * C], BF16, name="da", tag="da", align_bytes=64, bufs=8)
                 nc.scalar.copy(
-                    da[:].bitcast(F32).rearrange("p (s u) -> p s u", u=2), back[:].rearrange("p u s -> p s u")
+                    da[e][:].bitcast(F32).rearrange("p (s u) -> p s u", u=2), back[:].rearrange("p u s -> p s u")
                 )
-                nc.vector.quantize_mx(out=codes[e][:].bitcast(FP8X4), scales=scales[e][:], in_=da[:])
+                quantize(e)
 
-        for e0, n in BANKS0:
-            products(0, e0, n)
+        for e in range(DIRECT, DIRECT + 2):
+            if e == DIRECT + 1:
+                prod = keep.tile([P, 4, C], F32, name="prod_last", tag="da_3", align_bytes=64)
+            else:
+                prod = ring.tile([P, 4, C], F32, name="prod", tag="prod")
+            gathers(prod, gated[e], e * C, C)
+            if e == DIRECT:
+                nc.scalar.activation(
+                    da[e][:].rearrange("p (s t) -> p s t", t=4), prod[:].rearrange("p t s -> p s t"), COPY, scale=2.0
+                )
+            else:
+                nc.vector.tensor_scalar_mul(
+                    da[e][:].rearrange("p (c i t) -> p c t i", i=4, t=4),
+                    prod[:].rearrange("p t (c i) -> p c t i", i=4),
+                    2.0,
+                )
+            quantize(e)
+
+        def on_scalar(dst, src):
+            nc.scalar.activation(dst, src, COPY)
+
+        for number, (e0, n) in zip((6, 5, 7), BANKS0):
+            products(0, e0, n, nc.vector.tensor_copy if e0 == E - 1 else on_scalar, number)
         for b in range(1, 4):
-            for e0, n in BANKS:
-                products(b, e0, n)
+            for number, (e0, n) in zip((5, 7), BANKS):
+                products(b, e0, n, on_scalar, number)
 
         for b in range(4):
-            pieces = TAIL if b == 3 else [(0, 256), (256, 256)]
+            rows = slice(b * P, (b + 1) * P)
             first = keep.tile([P, T], F32, name="first_%d" % b)
-            for t0, w in pieces:
-                nc.vector.tensor_copy(first[:, t0 : t0 + w], dx[b][:].indirect(pos1_t[:, t0 // 16 : (t0 + w) // 16]))
             total = keep.tile([P, T], F32, name="total_%d" % b)
-            for t0, w in pieces:
-                nc.vector.tensor_tensor(
-                    total[:, t0 : t0 + w],
-                    dx[b][:].indirect(pos2_t[:, t0 // 16 : (t0 + w) // 16]),
-                    first[:, t0 : t0 + w],
-                    ADD,
-                )
-                if b == 3:
-                    nc.sync.dma_start(out[b * P : (b + 1) * P, t0 : t0 + w], total[:, t0 : t0 + w])
             if b < 3:
-                nc.sync.dma_start(out[b * P : (b + 1) * P, :], total[:])
+                second = keep.tile([P, T], F32, name="second_%d" % b)
+                nc.vector.tensor_copy(first[:], dx[b][:].indirect(pos1_t[:]))
+                nc.vector.tensor_copy(second[:], dx[b][:].indirect(pos2_t[:]))
+                nc.gpsimd.tensor_tensor(total[:], first[:], second[:], ADD)
+                nc.sync.dma_start(out[rows, :], total[:])
+            else:
+                for t0, w in TAIL:
+                    nc.vector.tensor_copy(
+                        first[:, t0 : t0 + w], dx[b][:].indirect(pos1_t[:, t0 // 16 : (t0 + w) // 16])
+                    )
+                for t0, w in TAIL:
+                    nc.vector.tensor_tensor(
+                        total[:, t0 : t0 + w],
+                        dx[b][:].indirect(pos2_t[:, t0 // 16 : (t0 + w) // 16]),
+                        first[:, t0 : t0 + w],
+                        ADD,
+                    )
+                    nc.sync.dma_start(out[rows, t0 : t0 + w], total[:, t0 : t0 + w])

@@ -24,8 +24,10 @@ RELU = mybir.ActivationFunctionType.Relu
 
 DIRECT = 5
 A_LOADS = [(0, 2), (2, 2), (4, 1), (5, 2), (7, 1)]
-BANKS0 = [(0, 4), (4, 3), (7, 1)]
+BANKS0 = [(0, 4), (4, 2), (7, 1), (6, 1)]
+QUANTISED = [(0, 2), (2, 2), (4, 1), (5, 1), (6, 1), (7, 1)]
 BANKS = [(0, 4), (4, 4)]
+FIRST = [(0, 256), (256, 256)]
 TAIL = [(0, 256), (256, 128), (384, 128)]
 
 
@@ -121,16 +123,26 @@ def tile_moe_sdb_relu2_kernel(
                     start=True,
                     stop=True,
                 )
-                nc.scalar.activation(plane[:, n0 : n0 + w], acc[:, 0:w], COPY)
+                if t == 0 and n0 == 0:
+                    nc.vector.tensor_copy(plane[:, n0 : n0 + w], acc[:, 0:w])
+                else:
+                    nc.scalar.activation(plane[:, n0 : n0 + w], acc[:, 0:w], COPY)
             dc.append(plane)
 
         gate_ps = bank(7, [P, P])
         nc.tensor.transpose(gate_ps[:], gate_rows[:], ident[:])
         nc.scalar.activation(gate2[:], gate_ps[:, 0:E], COPY, scale=2.0)
 
-        codes = [keep.tile([P, C], U32, name="codes_%d" % e, align_bytes=64) for e in range(E)]
-        scales = [keep.tile([P, C], U8, name="scales_%d" % e, align_bytes=64) for e in range(E)]
-        da = [keep.tile([P, 4 * C], BF16, name="da_%d" % e, tag="da_%d" % e, align_bytes=64) for e in range(E)]
+        codes, scales, da, whole = {}, {}, {}, {}
+        for e0, n in QUANTISED:
+            words = keep.tile([P, n * C], U32, name="codes_%d" % e0, align_bytes=64)
+            plane = keep.tile([P, n * C], U8, name="scales_%d" % e0, align_bytes=64)
+            values = keep.tile([P, 4 * n * C], BF16, name="da_%d" % e0, tag="da_%d" % e0, align_bytes=64)
+            whole[e0] = (words, plane, values)
+            for j in range(n):
+                codes[e0 + j] = words[:, j * C : (j + 1) * C]
+                scales[e0 + j] = plane[:, j * C : (j + 1) * C]
+                da[e0 + j] = values[:, 4 * j * C : 4 * (j + 1) * C]
         dx = [keep.tile([P, S], F32, name="dx_%d" % b) for b in range(4)]
 
         def products(b, e0, n, evac, number):
@@ -140,8 +152,8 @@ def tile_moe_sdb_relu2_kernel(
                     out=acc[:, (e - e0) * C : (e - e0 + 1) * C],
                     lhsT=w1_w[:, e, 2 * P * b : 2 * P * (b + 1)].bitcast(FP4X4),
                     lhsT_scale=w1_s[:, e, P * b : P * (b + 1)],
-                    rhs=codes[e][:].bitcast(FP8X4),
-                    rhs_scale=scales[e][:],
+                    rhs=codes[e].bitcast(FP8X4),
+                    rhs_scale=scales[e],
                     start=True,
                     stop=True,
                 )
@@ -154,27 +166,29 @@ def tile_moe_sdb_relu2_kernel(
                 )
 
         def quantize(e):
-            nc.vector.quantize_mx(out=codes[e][:].bitcast(FP8X4), scales=scales[e][:], in_=da[e][:])
+            words, plane, values = whole[e]
+            nc.vector.quantize_mx(out=words[:].bitcast(FP8X4), scales=plane[:], in_=values[:])
 
-        gated = {}
-        for e0, n in [(5, 2)]:
-            tile = keep.tile([P, 4, n * C], F32, name="gated_%d" % e0)
-            cols = gate_cols[:, (e0 - DIRECT) * C : (e0 - DIRECT + n) * C]
+        factor_mixed = keep.tile([P, 4, 2 * C], F32, name="factor_mixed")
+        factor_last = keep.tile([P, 4, C], F32, name="factor_last")
+        for j, dst in enumerate((factor_mixed[:, :, C : 2 * C], factor_last[:])):
+            cols = gate_cols[:, j * C : (j + 1) * C]
             nc.vector.scalar_tensor_tensor(
-                tile[:], a_of(e0, n), 0.0, cols.unsqueeze(1).broadcast_to([P, 4, n * C]), MAX, MULT
+                dst, a_of(DIRECT + j, 1), 0.0, cols.unsqueeze(1).broadcast_to([P, 4, C]), MAX, MULT
             )
-            for e in range(e0, e0 + n):
-                gated[e] = [tile[:, t, (e - e0) * C : (e - e0 + 1) * C] for t in range(4)]
 
         for e0, n in [(0, 2), (2, 2), (4, 1), (7, 1)]:
-            pos = keep.tile([P, 4, n * C], F32, name="pos_%d" % e0)
+            mixed = e0 == DIRECT - 1
+            factor = factor_mixed if mixed else keep.tile([P, 4, n * C], F32, name="pos_%d" % e0)
+            pos = factor[:, :, 0 : n * C]
+            width = 2 * C if mixed else n * C
             for h, w in [(0, 2), (2, 2)] if n == 2 else [(0, 4)]:
                 if e0 in (0,):
                     nc.vector.tensor_scalar_max(pos[:, h : h + w, :], a_of(e0, n)[:, h : h + w, :], 0.0)
                 else:
                     nc.scalar.activation(pos[:, h : h + w, :], a_of(e0, n)[:, h : h + w, :], RELU)
-            prod = ring.tile([P, 4, n * C], F32, name="prod", tag="prod")
-            gathers(prod, [pos[:, t, :] for t in range(4)], e0 * C, n * C)
+            prod = ring.tile([P, 4, width], F32, name="prod", tag="prod")
+            gathers(prod, [factor[:, t, :] for t in range(4)], e0 * C, width)
             for e in range(e0, e0 + n):
                 j = e - e0
                 turned = bank(4 + e % 2, [P, H])
@@ -192,32 +206,35 @@ def tile_moe_sdb_relu2_kernel(
                 for u in range(2):
                     nc.tensor.transpose(back[:, u, :], words[:, u * P : (u + 1) * P], ident[:])
                 nc.scalar.copy(
-                    da[e][:].bitcast(F32).rearrange("p (s u) -> p s u", u=2), back[:].rearrange("p u s -> p s u")
+                    da[e].bitcast(F32).rearrange("p (s u) -> p s u", u=2), back[:].rearrange("p u s -> p s u")
                 )
-                quantize(e)
-
-        for e in range(DIRECT, DIRECT + 2):
-            if e == DIRECT + 1:
-                prod = keep.tile([P, 4, C], F32, name="prod_last", tag="da_3", align_bytes=64)
-            else:
-                prod = ring.tile([P, 4, C], F32, name="prod", tag="prod")
-            gathers(prod, gated[e], e * C, C)
-            if e == DIRECT:
+                if e in (1, 3):
+                    quantize(e - 1)
+                elif e > 3:
+                    quantize(e)
+            if mixed:
                 nc.scalar.activation(
-                    da[e][:].rearrange("p (s t) -> p s t", t=4), prod[:].rearrange("p t s -> p s t"), COPY, scale=2.0
+                    da[DIRECT].rearrange("p (s t) -> p s t", t=4),
+                    prod[:, :, C : 2 * C].rearrange("p t s -> p s t"),
+                    COPY,
+                    scale=2.0,
                 )
-            else:
-                nc.vector.tensor_scalar_mul(
-                    da[e][:].rearrange("p (c i t) -> p c t i", i=4, t=4),
-                    prod[:].rearrange("p t (c i) -> p c t i", i=4),
-                    2.0,
-                )
-            quantize(e)
+                quantize(DIRECT)
+
+        last = DIRECT + 1
+        prod = keep.tile([P, 4, C], F32, name="prod_last", tag="da_2", align_bytes=64)
+        gathers(prod, [factor_last[:, t, :] for t in range(4)], last * C, C)
+        nc.vector.tensor_scalar_mul(
+            da[last].rearrange("p (c i t) -> p c t i", i=4, t=4),
+            prod[:].rearrange("p t (c i) -> p c t i", i=4),
+            2.0,
+        )
+        quantize(last)
 
         def on_scalar(dst, src):
             nc.scalar.activation(dst, src, COPY)
 
-        for number, (e0, n) in zip((6, 5, 7), BANKS0):
+        for number, (e0, n) in zip((6, 4, 7, 5), BANKS0):
             products(0, e0, n, nc.vector.tensor_copy if e0 == E - 1 else on_scalar, number)
         for b in range(1, 4):
             for number, (e0, n) in zip((5, 7), BANKS):
@@ -234,7 +251,7 @@ def tile_moe_sdb_relu2_kernel(
                 nc.gpsimd.tensor_tensor(total[:], first[:], second[:], ADD)
                 nc.sync.dma_start(out[rows, :], total[:])
             else:
-                for t0, w in TAIL:
+                for t0, w in FIRST:
                     nc.vector.tensor_copy(
                         first[:, t0 : t0 + w], dx[b][:].indirect(pos1_t[:, t0 // 16 : (t0 + w) // 16])
                     )

@@ -22,13 +22,14 @@ MAX = mybir.AluOpType.max
 COPY = mybir.ActivationFunctionType.Copy
 RELU = mybir.ActivationFunctionType.Relu
 
-DIRECT = 5
-A_LOADS = [(0, 2), (2, 2), (4, 1), (5, 2), (7, 1)]
-BANKS0 = [(0, 4), (4, 2), (7, 1), (6, 1)]
-QUANTISED = [(0, 2), (2, 2), (4, 1), (5, 1), (6, 1), (7, 1)]
-BANKS = [(0, 4), (4, 4)]
-FIRST = [(0, 256), (256, 256)]
+TURNED = 6
+TURN_BANKS = [[0,4,1,2,3,0],[2,3,0,3,0,5]]
+BLOCK0 = [[0,2,5],[2,2,6],[4,2,1],[6,2,7]]
+BANKS = [[6,3],[7,4],[1,4]]
+HOLDS = {(4, 0): 3 * C // 2, (1, 1): 11 * C // 2}
+HALVES = [(0, 256), (256, 256)]
 TAIL = [(0, 256), (256, 128), (384, 128)]
+SHARE = 80
 
 
 def tile_moe_sdb_relu2_kernel(
@@ -37,7 +38,6 @@ def tile_moe_sdb_relu2_kernel(
     nc = tc.nc
     with ExitStack() as ctx:
         keep = ctx.enter_context(tc.tile_pool(name="keep", bufs=1))
-        ring = ctx.enter_context(tc.tile_pool(name="ring", bufs=2))
         psum = ctx.enter_context(tc.psum_pool(name="psum", bufs=1))
 
         def bank(number, shape):
@@ -50,14 +50,16 @@ def tile_moe_sdb_relu2_kernel(
         head_s = keep.tile([P, T + H], U8, name="head_s", align_bytes=64)
         w2_raw = keep.tile([P, 2 * H], U8, name="w2_raw", align_bytes=64)
         w2_w = keep.tile([P, 2 * H], U8, name="w2_w", align_bytes=64)
-        w2_s = keep.tile([P, H], U8, name="w2_s", align_bytes=64)
-        w1_w = keep.tile([P, E, 2 * K], U8, name="w1_w", align_bytes=64)
+        w2_s = [keep.tile([P, H // 2], U8, name="w2_s_%d" % h, tag="w2_s_%d" % h, align_bytes=64) for h in range(2)]
+        w1_w = keep.tile([P, E, 2 * K], U8, name="w1_w", tag="w1_w", align_bytes=64)
         w1_s = keep.tile([P, E, K], U8, name="w1_s", align_bytes=64)
         ident = keep.tile([P, P], F32, name="ident")
         gate_rows = keep.tile([P, C], F32, name="gate_rows")
         gate2 = keep.tile([P, E], F32, name="gate2")
-        direct = 2 * C
-        gate_cols = keep.tile([P, direct], F32, name="gate_cols")
+        gate_cols = keep.tile([P, 2 * C], F32, name="gate_cols")
+        a_direct = keep.tile([P, 4, 2 * C], F32, name="a_direct")
+        a_low = [keep.tile([P, 2, 3 * C], F32, name="a_low_%d" % g) for g in range(2)]
+        a_high = keep.tile([P, 2, TURNED * C], F32, name="a_high")
 
         nc.gpsimd.memset(head_s[:].bitcast(I32), 0)
         nc.vector.memset(gate_rows[:], 0.0)
@@ -65,32 +67,19 @@ def tile_moe_sdb_relu2_kernel(
         make_identity(nc, ident[:])
 
         a_planes = a.rearrange("(p t) s -> p t s", t=4)
-        a_tiles = [keep.tile([P, 4, n * C], F32, name="a_%d" % e0) for e0, n in A_LOADS]
-
-        def load_a(g):
-            e0, n = A_LOADS[g]
-            nc.sync.dma_start(a_tiles[g][:], a_planes[:, :, e0 * C : (e0 + n) * C])
-
-        def a_of(e, n):
-            g = max(i for i, (e0, count) in enumerate(A_LOADS) if e0 <= e)
-            j = e - A_LOADS[g][0]
-            return a_tiles[g][:, :, j * C : (j + n) * C]
-
         nc.sync.dma_start(w2_raw[:].bitcast(I32), w2t_words[0].bitcast(I32))
         nc.sync.dma_start(dy_w[:].bitcast(I32), dy_words[0].rearrange("p t d -> p (t d)").bitcast(I32))
         for r in range(4):
             nc.sync.dma_start(head_s[r:P:32, T : T + H].bitcast(I32), w2t_scales[0, r:16:4, :].bitcast(I32))
-        nc.sync.dma_start(gate_cols[:], gate[:, DIRECT * C : (DIRECT + 2) * C])
-        load_a(3)
+        nc.sync.dma_start(gate_cols[:], gate[:, TURNED * C : S])
+        nc.sync.dma_start(a_direct[:], a_planes[:, :, TURNED * C : S])
         for r in range(4):
             nc.sync.dma_start(head_s[r:P:32, 0:T].bitcast(I32), dy_scales[0, r:16:4, :].bitcast(I32))
+        nc.sync.dma_start(a_low[0][:], a_planes[:, 0:2, 0 : 3 * C])
         nc.sync.dma_start(offs_t[:], offs)
-        for h in range(0, 4, 2):
-            nc.sync.dma_start(a_tiles[0][:, h : h + 2, :], a_planes[:, h : h + 2, 0 : 2 * C])
-        load_a(1)
+        nc.sync.dma_start(a_low[1][:], a_planes[:, 0:2, 3 * C : 6 * C])
         nc.sync.dma_start(gate_rows[0:E, :], gate[0].rearrange("(e u) -> e u", u=C))
-        load_a(4)
-        load_a(2)
+        nc.sync.dma_start(a_high[:], a_planes[:, 2:4, 0 : TURNED * C])
         nc.sync.dma_start(w1_w[:].bitcast(I32), w1t_words.rearrange("e o p n -> p (e o) n").bitcast(I32))
         for r in range(4):
             nc.sync.dma_start(
@@ -104,48 +93,84 @@ def tile_moe_sdb_relu2_kernel(
             w2_w[:].bitcast(U16).rearrange("p (t m) -> p t m", t=4),
             w2_raw[:].bitcast(U16).rearrange("p (m t) -> p t m", t=4),
         )
-        nc.vector.tensor_copy(
-            w2_s[:].rearrange("p (t m) -> p t m", t=4),
-            head_s[:, T : T + H].rearrange("p (m t) -> p t m", t=4),
-        )
+        for h in range(2):
+            nc.vector.tensor_copy(
+                w2_s[h][:].rearrange("p (t m) -> p t m", t=2),
+                head_s[:, T : T + H].rearrange("p (m t) -> p t m", t=4)[:, 2 * h : 2 * h + 2, :],
+            )
 
-        dc = []
-        for t in range(4):
-            plane = keep.tile([P, T], F32, name="dc_%d" % t)
-            for n0, w in [(0, T // 2), (T // 2, T // 2)] if t == 0 else [(0, T)]:
-                acc = bank(4 if n0 else t, [P, T])
-                nc.tensor.matmul_mx(
-                    out=acc[:, 0:w],
-                    lhsT=w2_w[:, 2 * P * t : 2 * P * (t + 1)].bitcast(FP4X4),
-                    lhsT_scale=w2_s[:, P * t : P * (t + 1)],
-                    rhs=dy_w[:, n0 : n0 + w].bitcast(FP8X4),
-                    rhs_scale=head_s[:, n0 : n0 + w],
-                    start=True,
-                    stop=True,
-                )
-                if t == 0 and n0 == 0:
-                    nc.vector.tensor_copy(plane[:, n0 : n0 + w], acc[:, 0:w])
-                else:
-                    nc.scalar.activation(plane[:, n0 : n0 + w], acc[:, 0:w], COPY)
-            dc.append(plane)
+        factor_direct = keep.tile([P, 4, 2 * C], F32, name="factor_direct")
+        for h in range(2):
+            nc.vector.scalar_tensor_tensor(
+                factor_direct[:, 2 * h : 2 * h + 2, :],
+                a_direct[:, 2 * h : 2 * h + 2, :],
+                0.0,
+                gate_cols[:].unsqueeze(1).broadcast_to([P, 2, 2 * C]),
+                MAX,
+                MULT,
+            )
 
-        gate_ps = bank(7, [P, P])
+        def relu(dst, src, on_vector):
+            if on_vector:
+                nc.vector.tensor_scalar_max(dst, src, 0.0)
+            else:
+                nc.scalar.activation(dst, src, RELU)
+
+        def on_scalar(dst, src):
+            nc.scalar.activation(dst, src, COPY)
+
+        dc = [keep.tile([P, T], F32, name="dc_%d" % t) for t in range(4)]
+
+        def first_product(t, n0, w, number, evac):
+            acc = bank(number, [P, T])
+            nc.tensor.matmul_mx(
+                out=acc[:, 0:w],
+                lhsT=w2_w[:, 2 * P * t : 2 * P * (t + 1)].bitcast(FP4X4),
+                lhsT_scale=w2_s[t // 2][:, P * (t % 2) : P * (t % 2 + 1)],
+                rhs=dy_w[:, n0 : n0 + w].bitcast(FP8X4),
+                rhs_scale=head_s[:, n0 : n0 + w],
+                start=True,
+                stop=True,
+            )
+            evac(dc[t][:, n0 : n0 + w], acc[:, 0:w])
+
+        pos_low = [keep.tile([P, 2, 3 * C], F32, name="pos_low_0", tag="pos_low_0")]
+        first_product(0, 0, T // 2, 0, on_scalar)
+        first_product(0, T // 2, T // 2, 4, on_scalar)
+        first_product(1, 0, T, 1, on_scalar)
+        for d in range(2):
+            relu(pos_low[0][:, d, :], a_low[0][:, d, :], True)
+        pos_low.append(keep.tile([P, 2, 3 * C], F32, name="pos_low_1", tag="w2_s_0", align_bytes=64))
+        relu(pos_low[1][:], a_low[1][:], False)
+        first_product(2, 0, T, 2, on_scalar)
+        first_product(3, 0, T, 3, on_scalar)
+
+        arena = keep.tile([P, 8 * C], F32, name="arena", align_bytes=64)
+        pos_high = [
+            keep.tile([P, 2, 3 * C], F32, name="pos_high_0")[:],
+            keep.tile([P, 2, 3 * C], F32, name="pos_high_1")[:],
+        ]
+
+        def relu_high(g, on_vector):
+            relu(pos_high[g], a_high[:, :, 3 * g * C : 3 * (g + 1) * C], on_vector)
+
+        relu_high(0, False)
+        gate_ps = bank(5, [P, P])
         nc.tensor.transpose(gate_ps[:], gate_rows[:], ident[:])
         nc.scalar.activation(gate2[:], gate_ps[:, 0:E], COPY, scale=2.0)
 
-        codes, scales, da, whole = {}, {}, {}, {}
-        for e0, n in QUANTISED:
-            words = keep.tile([P, n * C], U32, name="codes_%d" % e0, align_bytes=64)
+        codes, scales = {}, {}
+        dx = [keep.tile([P, S], F32, name="dx_%d" % b) for b in range(4)]
+
+        def quantize(e0, n, values, tag):
+            words = keep.tile([P, n * C], U32, name="codes_%d" % e0, tag=tag, align_bytes=64)
             plane = keep.tile([P, n * C], U8, name="scales_%d" % e0, align_bytes=64)
-            values = keep.tile([P, 4 * n * C], BF16, name="da_%d" % e0, tag="da_%d" % e0, align_bytes=64)
-            whole[e0] = (words, plane, values)
+            nc.vector.quantize_mx(out=words[:].bitcast(FP8X4), scales=plane[:], in_=values)
             for j in range(n):
                 codes[e0 + j] = words[:, j * C : (j + 1) * C]
                 scales[e0 + j] = plane[:, j * C : (j + 1) * C]
-                da[e0 + j] = values[:, 4 * j * C : 4 * (j + 1) * C]
-        dx = [keep.tile([P, S], F32, name="dx_%d" % b) for b in range(4)]
 
-        def products(b, e0, n, evac, number):
+        def products(b, e0, n, number, engine="s"):
             acc = bank(number, [P, T])
             for e in range(e0, e0 + n):
                 nc.tensor.matmul_mx(
@@ -157,109 +182,98 @@ def tile_moe_sdb_relu2_kernel(
                     start=True,
                     stop=True,
                 )
+            evac = nc.vector.tensor_copy if engine == "v" else on_scalar
             evac(dx[b][:, e0 * C : (e0 + n) * C], acc[:, 0 : n * C])
 
-        def gathers(prod, factor, s0, w):
-            for t in range(4):
-                nc.vector.tensor_tensor(
-                    prod[:, t, :], dc[t][:].indirect(offs_t[:, s0 // 16 : (s0 + w) // 16]), factor[t], MULT
-                )
+        def gather(dst, t, s0, w, factor):
+            nc.vector.tensor_tensor(dst, dc[t][:].indirect(offs_t[:, s0 // 16 : (s0 + w) // 16]), factor, MULT)
 
-        def quantize(e):
-            words, plane, values = whole[e]
-            nc.vector.quantize_mx(out=words[:].bitcast(FP8X4), scales=plane[:], in_=values[:])
+        back = [None] * 3
 
-        factor_mixed = keep.tile([P, 4, 2 * C], F32, name="factor_mixed")
-        factor_last = keep.tile([P, 4, C], F32, name="factor_last")
-        for j, dst in enumerate((factor_mixed[:, :, C : 2 * C], factor_last[:])):
-            cols = gate_cols[:, j * C : (j + 1) * C]
-            nc.vector.scalar_tensor_tensor(
-                dst, a_of(DIRECT + j, 1), 0.0, cols.unsqueeze(1).broadcast_to([P, 4, C]), MAX, MULT
-            )
+        def half_turn(e, u, prod):
+            turned = bank(TURN_BANKS[u][e], [P, 2, P])
+            for d in range(2):
+                nc.tensor.transpose(turned[:, d, :], prod[:, d, :], ident[:])
+            if (e, u) in HOLDS:
+                x0 = HOLDS[e, u]
+                rows = arena[:, x0 : x0 + C].bitcast(BF16).rearrange("s (p d) -> s p d", d=2)
+            else:
+                rows = keep.tile(
+                    [P, P, 2], BF16, name="rows_%d_%d" % (e, u), tag="rows_%d_%d" % (e, u), align_bytes=64
+                )
+            nc.scalar.activation(rows[:], turned[:].rearrange("s d p -> s p d"), COPY, scale=gate2[:, e : e + 1])
+            if back[e // 2] is None:
+                back[e // 2] = bank(5 + e // 2, [P, 2, 2, C])
+            words = rows[:].rearrange("s p d -> s (p d)").bitcast(F32)
+            nc.tensor.transpose(back[e // 2][:, e % 2, u, :], words, ident[:])
 
-        for e0, n in [(0, 2), (2, 2), (4, 1), (7, 1)]:
-            mixed = e0 == DIRECT - 1
-            factor = factor_mixed if mixed else keep.tile([P, 4, n * C], F32, name="pos_%d" % e0)
-            pos = factor[:, :, 0 : n * C]
-            width = 2 * C if mixed else n * C
-            for h, w in [(0, 2), (2, 2)] if n == 2 else [(0, 4)]:
-                if e0 in (0,):
-                    nc.vector.tensor_scalar_max(pos[:, h : h + w, :], a_of(e0, n)[:, h : h + w, :], 0.0)
-                else:
-                    nc.scalar.activation(pos[:, h : h + w, :], a_of(e0, n)[:, h : h + w, :], RELU)
-            prod = ring.tile([P, 4, width], F32, name="prod", tag="prod")
-            gathers(prod, [factor[:, t, :] for t in range(4)], e0 * C, width)
-            for e in range(e0, e0 + n):
-                j = e - e0
-                turned = bank(4 + e % 2, [P, H])
-                for t in range(4):
-                    nc.tensor.transpose(turned[:, t * P : (t + 1) * P], prod[:, t, j * C : (j + 1) * C], ident[:])
-                da_rows = ring.tile([P, 2, P, 2], BF16, name="da_rows", tag="da_rows")
-                nc.scalar.activation(
-                    da_rows[:],
-                    turned[:].rearrange("s (u d p) -> s u p d", u=2, d=2),
-                    COPY,
-                    scale=gate2[:, e : e + 1],
-                )
-                words = da_rows[:].rearrange("s u p d -> s (u p d)").bitcast(F32)
-                back = bank(6 + e % 2, [P, 2, C])
-                for u in range(2):
-                    nc.tensor.transpose(back[:, u, :], words[:, u * P : (u + 1) * P], ident[:])
-                nc.scalar.copy(
-                    da[e].bitcast(F32).rearrange("p (s u) -> p s u", u=2), back[:].rearrange("p u s -> p s u")
-                )
-                if e in (1, 3):
-                    quantize(e - 1)
-                elif e > 3:
-                    quantize(e)
-            if mixed:
-                nc.scalar.activation(
-                    da[DIRECT].rearrange("p (s t) -> p s t", t=4),
-                    prod[:, :, C : 2 * C].rearrange("p t s -> p s t"),
-                    COPY,
-                    scale=2.0,
-                )
-                quantize(DIRECT)
+        for g in range(2):
+            prod = keep.tile([P, 2, 3 * C], F32, name="prod_low_%d" % g)
+            for d in range(2):
+                gather(prod[:, d, :], d, 3 * g * C, 3 * C, pos_low[g][:, d, :])
+            for j in range(3):
+                e = 3 * g + j
+                half_turn(e, 0, prod[:, :, j * C : (j + 1) * C])
+                if e == 1:
+                    relu_high(1, False)
 
-        last = DIRECT + 1
-        prod = keep.tile([P, 4, C], F32, name="prod_last", tag="da_2", align_bytes=64)
-        gathers(prod, [factor_last[:, t, :] for t in range(4)], last * C, C)
+        for g in range(2):
+            prod = keep.tile([P, 2, 3 * C], F32, name="prod_high_%d" % g)
+            for d in range(2):
+                gather(prod[:, d, :], 2 + d, 3 * g * C, 3 * C, pos_high[g][:, d, :])
+            for j in range(3):
+                e = 3 * g + j
+                half_turn(e, 1, prod[:, :, j * C : (j + 1) * C])
+                if e % 2:
+                    pair = keep.tile([P, 8 * C], BF16, name="da_%d" % (e - 1), align_bytes=64)
+                    nc.scalar.copy(
+                        pair[:].bitcast(F32).rearrange("p (e s u) -> p e s u", e=2, u=2),
+                        back[e // 2][:].rearrange("p e u s -> p e s u"),
+                    )
+                    quantize(e - 1, 2, pair[:], "codes_%d" % (e - 1))
+
+        planes = arena[:].rearrange("p (t s) -> p t s", t=4)
+        for t in range(4):
+            gather(planes[:, t, :], t, TURNED * C, 2 * C, factor_direct[:, t, :])
+        da_direct = keep.tile([P, 8 * C], BF16, name="da_direct", tag="rows_4_1", align_bytes=64)
         nc.vector.tensor_scalar_mul(
-            da[last].rearrange("p (c i t) -> p c t i", i=4, t=4),
-            prod[:].rearrange("p t (c i) -> p c t i", i=4),
+            da_direct[:].rearrange("p (c i t) -> p c t i", i=4, t=4),
+            planes.rearrange("p t (c i) -> p c t i", i=4),
             2.0,
         )
-        quantize(last)
+        quantize(TURNED, 2, da_direct[:], "codes_6")
 
-        def on_scalar(dst, src):
-            nc.scalar.activation(dst, src, COPY)
-
-        for number, (e0, n) in zip((6, 4, 7, 5), BANKS0):
-            products(0, e0, n, nc.vector.tensor_copy if e0 == E - 1 else on_scalar, number)
+        for entry in BLOCK0:
+            products(0, *entry)
         for b in range(1, 4):
-            for number, (e0, n) in zip((5, 7), BANKS):
-                products(b, e0, n, on_scalar, number)
+            for h in range(2):
+                products(b, 4 * h, 4, BANKS[b - 1][h])
 
-        for b in range(4):
-            rows = slice(b * P, (b + 1) * P)
-            first = keep.tile([P, T], F32, name="first_%d" % b)
-            total = keep.tile([P, T], F32, name="total_%d" % b)
-            if b < 3:
-                second = keep.tile([P, T], F32, name="second_%d" % b)
-                nc.vector.tensor_copy(first[:], dx[b][:].indirect(pos1_t[:]))
-                nc.vector.tensor_copy(second[:], dx[b][:].indirect(pos2_t[:]))
-                nc.gpsimd.tensor_tensor(total[:], first[:], second[:], ADD)
-                nc.sync.dma_start(out[rows, :], total[:])
-            else:
-                for t0, w in FIRST:
-                    nc.vector.tensor_copy(
-                        first[:, t0 : t0 + w], dx[b][:].indirect(pos1_t[:, t0 // 16 : (t0 + w) // 16])
-                    )
-                for t0, w in TAIL:
-                    nc.vector.tensor_tensor(
-                        total[:, t0 : t0 + w],
-                        dx[b][:].indirect(pos2_t[:, t0 // 16 : (t0 + w) // 16]),
-                        first[:, t0 : t0 + w],
-                        ADD,
-                    )
-                    nc.sync.dma_start(out[rows, t0 : t0 + w], total[:, t0 : t0 + w])
+        first = [keep.tile([P, T], F32, name="first_%d" % b) for b in range(4)]
+
+        def fetch_first(b, pieces):
+            for t0, w in pieces:
+                nc.vector.tensor_copy(first[b][:, t0 : t0 + w], dx[b][:].indirect(pos1_t[:, t0 // 16 : (t0 + w) // 16]))
+
+        def add_second(b, pieces, tag, piecewise):
+            total = keep.tile([P, T], F32, name="total_%d" % b, tag=tag, align_bytes=64)
+            for t0, w in pieces:
+                nc.vector.tensor_tensor(
+                    total[:, t0 : t0 + w],
+                    dx[b][:].indirect(pos2_t[:, t0 // 16 : (t0 + w) // 16]),
+                    first[b][:, t0 : t0 + w],
+                    ADD,
+                )
+                if piecewise:
+                    nc.sync.dma_start(out[b * P : (b + 1) * P, t0 : t0 + w], total[:, t0 : t0 + w])
+            if not piecewise:
+                nc.sync.dma_start(out[b * P : (b + 1) * P, :], total[:])
+
+        fetch_first(0, HALVES)
+        add_second(0, HALVES, "total_0", False)
+        fetch_first(1, [(0, T)])
+        fetch_first(2, [(0, T)])
+        add_second(1, [(0, T)], "w1_w", False)
+        add_second(2, [(0, T)], "total_2", False)
+        fetch_first(3, HALVES)
+        add_second(3, TAIL, "total_3", True)

@@ -23,13 +23,16 @@ COPY = mybir.ActivationFunctionType.Copy
 RELU = mybir.ActivationFunctionType.Relu
 
 TURNED = 6
-TURN_BANKS = [[0,4,1,2,3,0],[2,3,0,3,0,5]]
-BLOCK0 = [[0,2,5],[2,2,6],[4,2,1],[6,2,7]]
-BANKS = [[6,3],[7,4],[1,4]]
-HOLDS = {(4, 0): 3 * C // 2, (1, 1): 11 * C // 2}
-HALVES = [(0, 256), (256, 256)]
-TAIL = [(0, 256), (256, 128), (384, 128)]
-SHARE = 80
+DIRECT = E - TURNED
+TRIO = 3
+
+BACK = 5
+TURN_BANKS = [[0, 4, 1, 2, 3, 0], [2, 3, 0, 3, 0, BACK]]
+BLOCK0 = [(0, BACK), (2, BACK + 1), (4, 1), (TURNED, BACK + 2)]
+BLOCK_BANKS = [(BACK + 1, 3), (BACK + 2, 4), (1, 4)]
+WHOLE = [(0, T)]
+HALVES = [(0, T // 2), (T // 2, T // 2)]
+TAIL = [(0, T // 2), (T // 2, T // 4), (3 * T // 4, T // 4)]
 
 
 def tile_moe_sdb_relu2_kernel(
@@ -54,11 +57,11 @@ def tile_moe_sdb_relu2_kernel(
         w1_w = keep.tile([P, E, 2 * K], U8, name="w1_w", tag="w1_w", align_bytes=64)
         w1_s = keep.tile([P, E, K], U8, name="w1_s", align_bytes=64)
         ident = keep.tile([P, P], F32, name="ident")
-        gate_rows = keep.tile([P, C], F32, name="gate_rows")
-        gate2 = keep.tile([P, E], F32, name="gate2")
-        gate_cols = keep.tile([P, 2 * C], F32, name="gate_cols")
-        a_direct = keep.tile([P, 4, 2 * C], F32, name="a_direct")
-        a_low = [keep.tile([P, 2, 3 * C], F32, name="a_low_%d" % g) for g in range(2)]
+        gate_rows = keep.tile([P, TRIO, C], F32, name="gate_rows")
+        gate2 = keep.tile([P, 2, TRIO], F32, name="gate2")
+        gate_cols = keep.tile([P, DIRECT * C], F32, name="gate_cols")
+        a_direct = keep.tile([P, 4, DIRECT * C], F32, name="a_direct")
+        a_low = [keep.tile([P, 2, TRIO * C], F32, name="a_low_%d" % g) for g in range(2)]
         a_high = keep.tile([P, 2, TURNED * C], F32, name="a_high")
 
         nc.gpsimd.memset(head_s[:].bitcast(I32), 0)
@@ -75,10 +78,10 @@ def tile_moe_sdb_relu2_kernel(
         nc.sync.dma_start(a_direct[:], a_planes[:, :, TURNED * C : S])
         for r in range(4):
             nc.sync.dma_start(head_s[r:P:32, 0:T].bitcast(I32), dy_scales[0, r:16:4, :].bitcast(I32))
-        nc.sync.dma_start(a_low[0][:], a_planes[:, 0:2, 0 : 3 * C])
+        nc.sync.dma_start(a_low[0][:], a_planes[:, 0:2, 0 : TRIO * C])
         nc.sync.dma_start(offs_t[:], offs)
-        nc.sync.dma_start(a_low[1][:], a_planes[:, 0:2, 3 * C : 6 * C])
-        nc.sync.dma_start(gate_rows[0:E, :], gate[0].rearrange("(e u) -> e u", u=C))
+        nc.sync.dma_start(a_low[1][:], a_planes[:, 0:2, TRIO * C : TURNED * C])
+        nc.sync.dma_start(gate_rows[0:2, :, :], gate[0, 0 : TURNED * C].rearrange("(g j u) -> g j u", g=2, u=C))
         nc.sync.dma_start(a_high[:], a_planes[:, 2:4, 0 : TURNED * C])
         nc.sync.dma_start(w1_w[:].bitcast(I32), w1t_words.rearrange("e o p n -> p (e o) n").bitcast(I32))
         for r in range(4):
@@ -99,29 +102,20 @@ def tile_moe_sdb_relu2_kernel(
                 head_s[:, T : T + H].rearrange("p (m t) -> p t m", t=4)[:, 2 * h : 2 * h + 2, :],
             )
 
-        factor_direct = keep.tile([P, 4, 2 * C], F32, name="factor_direct")
+        factor_direct = keep.tile([P, 4, DIRECT * C], F32, name="factor_direct")
         for h in range(2):
             nc.vector.scalar_tensor_tensor(
                 factor_direct[:, 2 * h : 2 * h + 2, :],
                 a_direct[:, 2 * h : 2 * h + 2, :],
                 0.0,
-                gate_cols[:].unsqueeze(1).broadcast_to([P, 2, 2 * C]),
+                gate_cols[:].unsqueeze(1).broadcast_to([P, 2, DIRECT * C]),
                 MAX,
                 MULT,
             )
 
-        def relu(dst, src, on_vector):
-            if on_vector:
-                nc.vector.tensor_scalar_max(dst, src, 0.0)
-            else:
-                nc.scalar.activation(dst, src, RELU)
-
-        def on_scalar(dst, src):
-            nc.scalar.activation(dst, src, COPY)
-
         dc = [keep.tile([P, T], F32, name="dc_%d" % t) for t in range(4)]
 
-        def first_product(t, n0, w, number, evac):
+        def first_product(t, n0, w, number):
             acc = bank(number, [P, T])
             nc.tensor.matmul_mx(
                 out=acc[:, 0:w],
@@ -132,45 +126,43 @@ def tile_moe_sdb_relu2_kernel(
                 start=True,
                 stop=True,
             )
-            evac(dc[t][:, n0 : n0 + w], acc[:, 0:w])
+            nc.scalar.activation(dc[t][:, n0 : n0 + w], acc[:, 0:w], COPY)
 
-        pos_low = [keep.tile([P, 2, 3 * C], F32, name="pos_low_0", tag="pos_low_0")]
-        first_product(0, 0, T // 2, 0, on_scalar)
-        first_product(0, T // 2, T // 2, 4, on_scalar)
-        first_product(1, 0, T, 1, on_scalar)
+        relu_low = [keep.tile([P, 2, TRIO * C], F32, name="relu_low_0")]
+        first_product(0, 0, T // 2, 0)
+        first_product(0, T // 2, T // 2, 4)
+        first_product(1, 0, T, 1)
         for d in range(2):
-            relu(pos_low[0][:, d, :], a_low[0][:, d, :], True)
-        pos_low.append(keep.tile([P, 2, 3 * C], F32, name="pos_low_1", tag="w2_s_0", align_bytes=64))
-        relu(pos_low[1][:], a_low[1][:], False)
-        first_product(2, 0, T, 2, on_scalar)
-        first_product(3, 0, T, 3, on_scalar)
+            nc.vector.tensor_scalar_max(relu_low[0][:, d, :], a_low[0][:, d, :], 0.0)
+        relu_low.append(keep.tile([P, 2, TRIO * C], F32, name="relu_low_1", tag="w2_s_0", align_bytes=64))
+        nc.scalar.activation(relu_low[1][:], a_low[1][:], RELU)
+        first_product(2, 0, T, 2)
+        first_product(3, 0, T, 3)
 
-        arena = keep.tile([P, 8 * C], F32, name="arena", align_bytes=64)
-        pos_high = [
-            keep.tile([P, 2, 3 * C], F32, name="pos_high_0")[:],
-            keep.tile([P, 2, 3 * C], F32, name="pos_high_1")[:],
-        ]
+        prod_direct = keep.tile([P, 4 * DIRECT * C], F32, name="prod_direct", align_bytes=64)
+        relu_high = [keep.tile([P, 2, TRIO * C], F32, name="relu_high_%d" % g) for g in range(2)]
 
-        def relu_high(g, on_vector):
-            relu(pos_high[g], a_high[:, :, 3 * g * C : 3 * (g + 1) * C], on_vector)
+        def make_relu_high(g):
+            nc.scalar.activation(relu_high[g][:], a_high[:, :, TRIO * g * C : TRIO * (g + 1) * C], RELU)
 
-        relu_high(0, False)
-        gate_ps = bank(5, [P, P])
-        nc.tensor.transpose(gate_ps[:], gate_rows[:], ident[:])
-        nc.scalar.activation(gate2[:], gate_ps[:, 0:E], COPY, scale=2.0)
+        make_relu_high(0)
+        gate_ps = bank(BACK, [P, TRIO, P])
+        for j in range(TRIO):
+            nc.tensor.transpose(gate_ps[:, j, :], gate_rows[:, j, :], ident[:])
+        nc.scalar.activation(gate2[:], gate_ps[:, :, 0:2].rearrange("s j g -> s g j"), COPY, scale=2.0)
 
         codes, scales = {}, {}
         dx = [keep.tile([P, S], F32, name="dx_%d" % b) for b in range(4)]
 
-        def quantize(e0, n, values, tag):
-            words = keep.tile([P, n * C], U32, name="codes_%d" % e0, tag=tag, align_bytes=64)
-            plane = keep.tile([P, n * C], U8, name="scales_%d" % e0, align_bytes=64)
-            nc.vector.quantize_mx(out=words[:].bitcast(FP8X4), scales=plane[:], in_=values)
-            for j in range(n):
+        def quantize_pair(e0, woven):
+            words = keep.tile([P, 2 * C], U32, name="codes_%d" % e0, align_bytes=64)
+            scale_bytes = keep.tile([P, 2 * C], U8, name="scales_%d" % e0, align_bytes=64)
+            nc.vector.quantize_mx(out=words[:].bitcast(FP8X4), scales=scale_bytes[:], in_=woven)
+            for j in range(2):
                 codes[e0 + j] = words[:, j * C : (j + 1) * C]
-                scales[e0 + j] = plane[:, j * C : (j + 1) * C]
+                scales[e0 + j] = scale_bytes[:, j * C : (j + 1) * C]
 
-        def products(b, e0, n, number, engine="s"):
+        def second_product(b, e0, n, number):
             acc = bank(number, [P, T])
             for e in range(e0, e0 + n):
                 nc.tensor.matmul_mx(
@@ -182,72 +174,73 @@ def tile_moe_sdb_relu2_kernel(
                     start=True,
                     stop=True,
                 )
-            evac = nc.vector.tensor_copy if engine == "v" else on_scalar
-            evac(dx[b][:, e0 * C : (e0 + n) * C], acc[:, 0 : n * C])
+            nc.scalar.activation(dx[b][:, e0 * C : (e0 + n) * C], acc[:, 0 : n * C], COPY)
 
         def gather(dst, t, s0, w, factor):
             nc.vector.tensor_tensor(dst, dc[t][:].indirect(offs_t[:, s0 // 16 : (s0 + w) // 16]), factor, MULT)
 
-        back = [None] * 3
+        plane_width = DIRECT * C
+        rows_in_prod_direct = {(4, 0): plane_width - C // 2, (1, 1): 3 * plane_width - C // 2}
+        back = {}
 
         def half_turn(e, u, prod):
             turned = bank(TURN_BANKS[u][e], [P, 2, P])
             for d in range(2):
                 nc.tensor.transpose(turned[:, d, :], prod[:, d, :], ident[:])
-            if (e, u) in HOLDS:
-                x0 = HOLDS[e, u]
-                rows = arena[:, x0 : x0 + C].bitcast(BF16).rearrange("s (p d) -> s p d", d=2)
+            if (e, u) in rows_in_prod_direct:
+                x0 = rows_in_prod_direct[e, u]
+                rows = prod_direct[:, x0 : x0 + C].bitcast(BF16).rearrange("s (p d) -> s p d", d=2)
             else:
                 rows = keep.tile(
                     [P, P, 2], BF16, name="rows_%d_%d" % (e, u), tag="rows_%d_%d" % (e, u), align_bytes=64
                 )
-            nc.scalar.activation(rows[:], turned[:].rearrange("s d p -> s p d"), COPY, scale=gate2[:, e : e + 1])
-            if back[e // 2] is None:
-                back[e // 2] = bank(5 + e // 2, [P, 2, 2, C])
+            scale = gate2[:, e // TRIO, e % TRIO : e % TRIO + 1]
+            nc.scalar.activation(rows[:], turned[:].rearrange("s d p -> s p d"), COPY, scale=scale)
+            if e // 2 not in back:
+                back[e // 2] = bank(BACK + e // 2, [P, 2, 2, C])
             words = rows[:].rearrange("s p d -> s (p d)").bitcast(F32)
             nc.tensor.transpose(back[e // 2][:, e % 2, u, :], words, ident[:])
 
         for g in range(2):
-            prod = keep.tile([P, 2, 3 * C], F32, name="prod_low_%d" % g)
+            prod = keep.tile([P, 2, TRIO * C], F32, name="prod_low_%d" % g)
             for d in range(2):
-                gather(prod[:, d, :], d, 3 * g * C, 3 * C, pos_low[g][:, d, :])
-            for j in range(3):
-                e = 3 * g + j
-                half_turn(e, 0, prod[:, :, j * C : (j + 1) * C])
-                if e == 1:
-                    relu_high(1, False)
+                gather(prod[:, d, :], d, TRIO * g * C, TRIO * C, relu_low[g][:, d, :])
+            for j in range(TRIO):
+                half_turn(TRIO * g + j, 0, prod[:, :, j * C : (j + 1) * C])
+                if (g, j) == (0, 1):
+                    make_relu_high(1)
 
         for g in range(2):
-            prod = keep.tile([P, 2, 3 * C], F32, name="prod_high_%d" % g)
+            prod = keep.tile([P, 2, TRIO * C], F32, name="prod_high_%d" % g)
             for d in range(2):
-                gather(prod[:, d, :], 2 + d, 3 * g * C, 3 * C, pos_high[g][:, d, :])
-            for j in range(3):
-                e = 3 * g + j
+                gather(prod[:, d, :], 2 + d, TRIO * g * C, TRIO * C, relu_high[g][:, d, :])
+            for j in range(TRIO):
+                e = TRIO * g + j
                 half_turn(e, 1, prod[:, :, j * C : (j + 1) * C])
                 if e % 2:
-                    pair = keep.tile([P, 8 * C], BF16, name="da_%d" % (e - 1), align_bytes=64)
+                    woven = keep.tile([P, 8 * C], BF16, name="da_%d" % (e - 1), align_bytes=64)
                     nc.scalar.copy(
-                        pair[:].bitcast(F32).rearrange("p (e s u) -> p e s u", e=2, u=2),
+                        woven[:].bitcast(F32).rearrange("p (e s u) -> p e s u", e=2, u=2),
                         back[e // 2][:].rearrange("p e u s -> p e s u"),
                     )
-                    quantize(e - 1, 2, pair[:], "codes_%d" % (e - 1))
+                    quantize_pair(e - 1, woven[:])
 
-        planes = arena[:].rearrange("p (t s) -> p t s", t=4)
+        planes_direct = prod_direct[:].rearrange("p (t s) -> p t s", t=4)
         for t in range(4):
-            gather(planes[:, t, :], t, TURNED * C, 2 * C, factor_direct[:, t, :])
-        da_direct = keep.tile([P, 8 * C], BF16, name="da_direct", tag="rows_4_1", align_bytes=64)
+            gather(planes_direct[:, t, :], t, TURNED * C, plane_width, factor_direct[:, t, :])
+        woven_direct = keep.tile([P, 4 * plane_width], BF16, name="da_direct", tag="rows_4_1", align_bytes=64)
         nc.vector.tensor_scalar_mul(
-            da_direct[:].rearrange("p (c i t) -> p c t i", i=4, t=4),
-            planes.rearrange("p t (c i) -> p c t i", i=4),
+            woven_direct[:].rearrange("p (c i t) -> p c t i", i=4, t=4),
+            planes_direct.rearrange("p t (c i) -> p c t i", i=4),
             2.0,
         )
-        quantize(TURNED, 2, da_direct[:], "codes_6")
+        quantize_pair(TURNED, woven_direct[:])
 
-        for entry in BLOCK0:
-            products(0, *entry)
+        for e0, number in BLOCK0:
+            second_product(0, e0, 2, number)
         for b in range(1, 4):
             for h in range(2):
-                products(b, 4 * h, 4, BANKS[b - 1][h])
+                second_product(b, 4 * h, 4, BLOCK_BANKS[b - 1][h])
 
         first = [keep.tile([P, T], F32, name="first_%d" % b) for b in range(4)]
 
@@ -255,25 +248,28 @@ def tile_moe_sdb_relu2_kernel(
             for t0, w in pieces:
                 nc.vector.tensor_copy(first[b][:, t0 : t0 + w], dx[b][:].indirect(pos1_t[:, t0 // 16 : (t0 + w) // 16]))
 
-        def add_second(b, pieces, tag, piecewise):
+        def add_second(b, total, t0, w):
+            nc.vector.tensor_tensor(
+                total[:, t0 : t0 + w],
+                dx[b][:].indirect(pos2_t[:, t0 // 16 : (t0 + w) // 16]),
+                first[b][:, t0 : t0 + w],
+                ADD,
+            )
+
+        def add_and_store(b, pieces, tag):
             total = keep.tile([P, T], F32, name="total_%d" % b, tag=tag, align_bytes=64)
             for t0, w in pieces:
-                nc.vector.tensor_tensor(
-                    total[:, t0 : t0 + w],
-                    dx[b][:].indirect(pos2_t[:, t0 // 16 : (t0 + w) // 16]),
-                    first[b][:, t0 : t0 + w],
-                    ADD,
-                )
-                if piecewise:
-                    nc.sync.dma_start(out[b * P : (b + 1) * P, t0 : t0 + w], total[:, t0 : t0 + w])
-            if not piecewise:
-                nc.sync.dma_start(out[b * P : (b + 1) * P, :], total[:])
+                add_second(b, total, t0, w)
+            nc.sync.dma_start(out[b * P : (b + 1) * P, :], total[:])
 
         fetch_first(0, HALVES)
-        add_second(0, HALVES, "total_0", False)
-        fetch_first(1, [(0, T)])
-        fetch_first(2, [(0, T)])
-        add_second(1, [(0, T)], "w1_w", False)
-        add_second(2, [(0, T)], "total_2", False)
+        add_and_store(0, HALVES, "total_0")
+        fetch_first(1, WHOLE)
+        fetch_first(2, WHOLE)
+        add_and_store(1, WHOLE, "w1_w")
+        add_and_store(2, WHOLE, "total_2")
         fetch_first(3, HALVES)
-        add_second(3, TAIL, "total_3", True)
+        total_last = keep.tile([P, T], F32, name="total_3", align_bytes=64)
+        for t0, w in TAIL:
+            add_second(3, total_last, t0, w)
+            nc.sync.dma_start(out[3 * P : 4 * P, t0 : t0 + w], total_last[:, t0 : t0 + w])

@@ -1,7 +1,6 @@
 from contextlib import ExitStack
 
 import concourse.mybir as mybir
-from concourse.masks import make_identity
 
 K, T, E, C, H, N = 512, 512, 8, 128, 512, 512
 S = E * C
@@ -22,14 +21,8 @@ MAX = mybir.AluOpType.max
 COPY = mybir.ActivationFunctionType.Copy
 RELU = mybir.ActivationFunctionType.Relu
 
-TURNED = 6
-DIRECT = E - TURNED
-TRIO = 3
-
-BACK = 5
-TURN_BANKS = [[0, 4, 1, 2, 3, 0], [2, 3, 0, 3, 0, BACK]]
-BLOCK0 = [(0, BACK), (2, BACK + 1), (4, 1), (TURNED, BACK + 2)]
-BLOCK_BANKS = [(BACK + 1, 3), (BACK + 2, 4), (1, 4)]
+GROUPS = [(0, 2), (2, 2), (4, 3), (7, 1)]
+OWN = 1
 WHOLE = [(0, T)]
 HALVES = [(0, T // 2), (T // 2, T // 2)]
 TAIL = [(0, T // 2), (T // 2, T // 4), (3 * T // 4, T // 4)]
@@ -43,8 +36,8 @@ def tile_moe_sdb_relu2_kernel(
         keep = ctx.enter_context(tc.tile_pool(name="keep", bufs=1))
         psum = ctx.enter_context(tc.psum_pool(name="psum", bufs=1))
 
-        def bank(number, shape):
-            return psum.tile(shape, F32, name="bank_%d" % number, tag="bank_%d" % number)
+        def bank(number):
+            return psum.tile([P, T], F32, name="bank_%d" % number, tag="bank_%d" % number)
 
         offs_t = keep.tile([P, S // 16], U16, name="offs_t")
         pos1_t = keep.tile([P, T // 16], U16, name="pos1_t")
@@ -53,36 +46,36 @@ def tile_moe_sdb_relu2_kernel(
         head_s = keep.tile([P, T + H], U8, name="head_s", align_bytes=64)
         w2_raw = keep.tile([P, 2 * H], U8, name="w2_raw", align_bytes=64)
         w2_w = keep.tile([P, 2 * H], U8, name="w2_w", align_bytes=64)
-        w2_s = [keep.tile([P, H // 2], U8, name="w2_s_%d" % h, tag="w2_s_%d" % h, align_bytes=64) for h in range(2)]
-        w1_w = keep.tile([P, E, 2 * K], U8, name="w1_w", tag="w1_w", align_bytes=64)
+        w2_s = keep.tile([P, H], U8, name="w2_s", align_bytes=64)
+        w1_w = keep.tile([P, E, 2 * K], U8, name="w1_w", align_bytes=64)
         w1_s = keep.tile([P, E, K], U8, name="w1_s", align_bytes=64)
-        ident = keep.tile([P, P], F32, name="ident")
-        gate_rows = keep.tile([P, TRIO, C], F32, name="gate_rows")
-        gate2 = keep.tile([P, 2, TRIO], F32, name="gate2")
-        gate_cols = keep.tile([P, DIRECT * C], F32, name="gate_cols")
-        a_direct = keep.tile([P, 4, DIRECT * C], F32, name="a_direct")
-        a_low = [keep.tile([P, 2, TRIO * C], F32, name="a_low_%d" % g) for g in range(2)]
-        a_high = keep.tile([P, 2, TURNED * C], F32, name="a_high")
+        first_width = GROUPS[0][1] * C
+        gate_first = keep.tile([P, first_width], F32, name="gate_first")
+        gate_rest = keep.tile([P, S - first_width], F32, name="gate_rest")
+        a_t = [keep.tile([P, 4, n * C], F32, name="a_%d" % g) for g, (e0, n) in enumerate(GROUPS)]
 
         nc.gpsimd.memset(head_s[:].bitcast(I32), 0)
-        nc.vector.memset(gate_rows[:], 0.0)
         nc.vector.memset(w1_s[:].rearrange("p e k -> p (e k)").bitcast(I32), 0)
-        make_identity(nc, ident[:])
 
         a_planes = a.rearrange("(p t) s -> p t s", t=4)
+
+        def load_a(g):
+            e0, n = GROUPS[g]
+            nc.sync.dma_start(a_t[g][:], a_planes[:, :, e0 * C : (e0 + n) * C])
+
         nc.sync.dma_start(w2_raw[:].bitcast(I32), w2t_words[0].bitcast(I32))
-        nc.sync.dma_start(dy_w[:].bitcast(I32), dy_words[0].rearrange("p t d -> p (t d)").bitcast(I32))
         for r in range(4):
             nc.sync.dma_start(head_s[r:P:32, T : T + H].bitcast(I32), w2t_scales[0, r:16:4, :].bitcast(I32))
-        nc.sync.dma_start(gate_cols[:], gate[:, TURNED * C : S])
-        nc.sync.dma_start(a_direct[:], a_planes[:, :, TURNED * C : S])
+        nc.sync.dma_start(gate_first[:], gate[:, 0:first_width])
+        load_a(0)
+        nc.sync.dma_start(dy_w[:].bitcast(I32), dy_words[0].rearrange("p t d -> p (t d)").bitcast(I32))
         for r in range(4):
             nc.sync.dma_start(head_s[r:P:32, 0:T].bitcast(I32), dy_scales[0, r:16:4, :].bitcast(I32))
-        nc.sync.dma_start(a_low[0][:], a_planes[:, 0:2, 0 : TRIO * C])
+        nc.sync.dma_start(gate_rest[:], gate[:, first_width:S])
         nc.sync.dma_start(offs_t[:], offs)
-        nc.sync.dma_start(a_low[1][:], a_planes[:, 0:2, TRIO * C : TURNED * C])
-        nc.sync.dma_start(gate_rows[0:2, :, :], gate[0, 0 : TURNED * C].rearrange("(g j u) -> g j u", g=2, u=C))
-        nc.sync.dma_start(a_high[:], a_planes[:, 2:4, 0 : TURNED * C])
+        load_a(1)
+        load_a(2)
+        load_a(3)
         nc.sync.dma_start(w1_w[:].bitcast(I32), w1t_words.rearrange("e o p n -> p (e o) n").bitcast(I32))
         for r in range(4):
             nc.sync.dma_start(
@@ -96,180 +89,179 @@ def tile_moe_sdb_relu2_kernel(
             w2_w[:].bitcast(U16).rearrange("p (t m) -> p t m", t=4),
             w2_raw[:].bitcast(U16).rearrange("p (m t) -> p t m", t=4),
         )
-        for h in range(2):
-            nc.vector.tensor_copy(
-                w2_s[h][:].rearrange("p (t m) -> p t m", t=2),
-                head_s[:, T : T + H].rearrange("p (m t) -> p t m", t=4)[:, 2 * h : 2 * h + 2, :],
-            )
+        nc.vector.tensor_copy(
+            w2_s[:].rearrange("p (t m) -> p t m", t=4),
+            head_s[:, T : T + H].rearrange("p (m t) -> p t m", t=4),
+        )
 
-        factor_direct = keep.tile([P, 4, DIRECT * C], F32, name="factor_direct")
-        for h in range(2):
+        def gate_cols(g):
+            e0, n = GROUPS[g]
+            if g == 0:
+                return gate_first[:]
+            return gate_rest[:, e0 * C - first_width : (e0 + n) * C - first_width]
+
+        def group_offs(g):
+            e0, n = GROUPS[g]
+            return offs_t[:, e0 * C // 16 : (e0 + n) * C // 16]
+
+        own_width = GROUPS[OWN][1] * C
+
+        factor = {}
+
+        def make_factor(g):
+            w = GROUPS[g][1] * C
+            factor[g] = keep.tile([P, 4, w], F32, name="factor_%d" % g)
             nc.vector.scalar_tensor_tensor(
-                factor_direct[:, 2 * h : 2 * h + 2, :],
-                a_direct[:, 2 * h : 2 * h + 2, :],
-                0.0,
-                gate_cols[:].unsqueeze(1).broadcast_to([P, 2, DIRECT * C]),
-                MAX,
-                MULT,
+                factor[g][:], a_t[g][:], 0.0, gate_cols(g).unsqueeze(1).broadcast_to([P, 4, w]), MAX, MULT
             )
 
         dc = [keep.tile([P, T], F32, name="dc_%d" % t) for t in range(4)]
 
         def first_product(t, n0, w, number):
-            acc = bank(number, [P, T])
+            acc = bank(number)
             nc.tensor.matmul_mx(
                 out=acc[:, 0:w],
                 lhsT=w2_w[:, 2 * P * t : 2 * P * (t + 1)].bitcast(FP4X4),
-                lhsT_scale=w2_s[t // 2][:, P * (t % 2) : P * (t % 2 + 1)],
+                lhsT_scale=w2_s[:, P * t : P * (t + 1)],
                 rhs=dy_w[:, n0 : n0 + w].bitcast(FP8X4),
                 rhs_scale=head_s[:, n0 : n0 + w],
                 start=True,
                 stop=True,
             )
-            nc.scalar.activation(dc[t][:, n0 : n0 + w], acc[:, 0:w], COPY)
+            nc.scalar.activation(dc[t][:, n0 : n0 + w], acc[:, 0:w], COPY, scale=2.0)
 
-        relu_low = [keep.tile([P, 2, TRIO * C], F32, name="relu_low_0")]
+        def leave_psum(dst, src, on_scalar):
+            if on_scalar:
+                nc.scalar.activation(dst, src, COPY)
+            else:
+                nc.vector.tensor_copy(dst, src)
+
+        make_factor(0)
         first_product(0, 0, T // 2, 0)
         first_product(0, T // 2, T // 2, 4)
-        first_product(1, 0, T, 1)
-        for d in range(2):
-            nc.vector.tensor_scalar_max(relu_low[0][:, d, :], a_low[0][:, d, :], 0.0)
-        relu_low.append(keep.tile([P, 2, TRIO * C], F32, name="relu_low_1", tag="w2_s_0", align_bytes=64))
-        nc.scalar.activation(relu_low[1][:], a_low[1][:], RELU)
-        first_product(2, 0, T, 2)
-        first_product(3, 0, T, 3)
+        for t in range(1, 4):
+            first_product(t, 0, T, t)
 
-        prod_direct = keep.tile([P, 4 * DIRECT * C], F32, name="prod_direct", align_bytes=64)
-        relu_high = [keep.tile([P, 2, TRIO * C], F32, name="relu_high_%d" % g) for g in range(2)]
+        picked = [keep.tile([P, 4, n * C], F32, name="picked_%d" % g) for g, (e0, n) in enumerate(GROUPS)]
+        for g in range(len(GROUPS)):
+            for t in range(4):
+                window = dc[t][:].indirect(group_offs(g))
+                if g == OWN:
+                    nc.vector.tensor_tensor(picked[g][:, t, :], window, gate_cols(g), MULT)
+                else:
+                    nc.scalar.activation(picked[g][:, t, :], window, COPY)
 
-        def make_relu_high(g):
-            nc.scalar.activation(relu_high[g][:], a_high[:, :, TRIO * g * C : TRIO * (g + 1) * C], RELU)
+        da = [keep.tile([P, 4 * n * C], BF16, name="da_%d" % g, align_bytes=64) for g, (e0, n) in enumerate(GROUPS)]
+        codes = keep.tile([P, S], U32, name="codes", align_bytes=64)
+        scales = keep.tile([P, S], U8, name="scales", align_bytes=64)
 
-        make_relu_high(0)
-        gate_ps = bank(BACK, [P, TRIO, P])
-        for j in range(TRIO):
-            nc.tensor.transpose(gate_ps[:, j, :], gate_rows[:, j, :], ident[:])
-        nc.scalar.activation(gate2[:], gate_ps[:, :, 0:2].rearrange("s j g -> s g j"), COPY, scale=2.0)
+        def make_da(g):
+            nc.vector.tensor_tensor(
+                da[g][:].rearrange("p (c i t) -> p c t i", i=2, t=4),
+                picked[g][:].rearrange("p t (c i) -> p c t i", i=2),
+                factor[g][:].rearrange("p t (c i) -> p c t i", i=2),
+                MULT,
+            )
 
-        codes, scales = {}, {}
+        pairs = keep.tile([P, 2, own_width, 2], BF16, name="pairs")
+
+        def make_pairs(u):
+            nc.vector.scalar_tensor_tensor(
+                pairs[:, u, :, :],
+                a_t[OWN][:, 2 * u : 2 * u + 2, :].rearrange("p d s -> p s d"),
+                0.0,
+                picked[OWN][:, 2 * u : 2 * u + 2, :].rearrange("p d s -> p s d"),
+                MAX,
+                MULT,
+            )
+
+        def weave_pairs():
+            nc.vector.tensor_copy(
+                da[OWN][:].bitcast(F32).rearrange("p (s u) -> p s u", u=2),
+                pairs[:].rearrange("p u s d -> p u (s d)").bitcast(F32).rearrange("p u s -> p s u"),
+            )
+
+        def quantize(g):
+            e0, n = GROUPS[g]
+            cols = slice(e0 * C, (e0 + n) * C)
+            nc.vector.quantize_mx(out=codes[:, cols].bitcast(FP8X4), scales=scales[:, cols], in_=da[g][:])
+
         dx = [keep.tile([P, S], F32, name="dx_%d" % b) for b in range(4)]
+        accs = {}
 
-        def quantize_pair(e0, woven):
-            words = keep.tile([P, 2 * C], U32, name="codes_%d" % e0, align_bytes=64)
-            scale_bytes = keep.tile([P, 2 * C], U8, name="scales_%d" % e0, align_bytes=64)
-            nc.vector.quantize_mx(out=words[:].bitcast(FP8X4), scales=scale_bytes[:], in_=woven)
-            for j in range(2):
-                codes[e0 + j] = words[:, j * C : (j + 1) * C]
-                scales[e0 + j] = scale_bytes[:, j * C : (j + 1) * C]
-
-        def second_product(b, e0, n, number):
-            acc = bank(number, [P, T])
-            for e in range(e0, e0 + n):
-                nc.tensor.matmul_mx(
-                    out=acc[:, (e - e0) * C : (e - e0 + 1) * C],
-                    lhsT=w1_w[:, e, 2 * P * b : 2 * P * (b + 1)].bitcast(FP4X4),
-                    lhsT_scale=w1_s[:, e, P * b : P * (b + 1)],
-                    rhs=codes[e].bitcast(FP8X4),
-                    rhs_scale=scales[e],
-                    start=True,
-                    stop=True,
-                )
-            nc.scalar.activation(dx[b][:, e0 * C : (e0 + n) * C], acc[:, 0 : n * C], COPY)
-
-        def gather(dst, t, s0, w, factor):
-            nc.vector.tensor_tensor(dst, dc[t][:].indirect(offs_t[:, s0 // 16 : (s0 + w) // 16]), factor, MULT)
-
-        plane_width = DIRECT * C
-        rows_in_prod_direct = {(4, 0): plane_width - C // 2, (1, 1): 3 * plane_width - C // 2}
-        back = {}
-
-        def half_turn(e, u, prod):
-            turned = bank(TURN_BANKS[u][e], [P, 2, P])
-            for d in range(2):
-                nc.tensor.transpose(turned[:, d, :], prod[:, d, :], ident[:])
-            if (e, u) in rows_in_prod_direct:
-                x0 = rows_in_prod_direct[e, u]
-                rows = prod_direct[:, x0 : x0 + C].bitcast(BF16).rearrange("s (p d) -> s p d", d=2)
-            else:
-                rows = keep.tile(
-                    [P, P, 2], BF16, name="rows_%d_%d" % (e, u), tag="rows_%d_%d" % (e, u), align_bytes=64
-                )
-            scale = gate2[:, e // TRIO, e % TRIO : e % TRIO + 1]
-            nc.scalar.activation(rows[:], turned[:].rearrange("s d p -> s p d"), COPY, scale=scale)
-            if e // 2 not in back:
-                back[e // 2] = bank(BACK + e // 2, [P, 2, 2, C])
-            words = rows[:].rearrange("s p d -> s (p d)").bitcast(F32)
-            nc.tensor.transpose(back[e // 2][:, e % 2, u, :], words, ident[:])
-
-        for g in range(2):
-            prod = keep.tile([P, 2, TRIO * C], F32, name="prod_low_%d" % g)
-            for d in range(2):
-                gather(prod[:, d, :], d, TRIO * g * C, TRIO * C, relu_low[g][:, d, :])
-            for j in range(TRIO):
-                half_turn(TRIO * g + j, 0, prod[:, :, j * C : (j + 1) * C])
-                if (g, j) == (0, 1):
-                    make_relu_high(1)
-
-        for g in range(2):
-            prod = keep.tile([P, 2, TRIO * C], F32, name="prod_high_%d" % g)
-            for d in range(2):
-                gather(prod[:, d, :], 2 + d, TRIO * g * C, TRIO * C, relu_high[g][:, d, :])
-            for j in range(TRIO):
-                e = TRIO * g + j
-                half_turn(e, 1, prod[:, :, j * C : (j + 1) * C])
-                if e % 2:
-                    woven = keep.tile([P, 8 * C], BF16, name="da_%d" % (e - 1), align_bytes=64)
-                    nc.scalar.copy(
-                        woven[:].bitcast(F32).rearrange("p (e s u) -> p e s u", e=2, u=2),
-                        back[e // 2][:].rearrange("p e u s -> p e s u"),
+        def second_product(g, blocks=range(4)):
+            e0, n = GROUPS[g]
+            for b in blocks:
+                key = (e0 // 4, b)
+                if key not in accs:
+                    accs[key] = bank(4 * (e0 // 4) + b)
+                for e in range(e0, e0 + n):
+                    nc.tensor.matmul_mx(
+                        out=accs[key][:, (e % 4) * C : (e % 4 + 1) * C],
+                        lhsT=w1_w[:, e, 2 * P * b : 2 * P * (b + 1)].bitcast(FP4X4),
+                        lhsT_scale=w1_s[:, e, P * b : P * (b + 1)],
+                        rhs=codes[:, e * C : (e + 1) * C].bitcast(FP8X4),
+                        rhs_scale=scales[:, e * C : (e + 1) * C],
+                        start=True,
+                        stop=True,
                     )
-                    quantize_pair(e - 1, woven[:])
 
-        planes_direct = prod_direct[:].rearrange("p (t s) -> p t s", t=4)
-        for t in range(4):
-            gather(planes_direct[:, t, :], t, TURNED * C, plane_width, factor_direct[:, t, :])
-        woven_direct = keep.tile([P, 4 * plane_width], BF16, name="da_direct", tag="rows_4_1", align_bytes=64)
-        nc.vector.tensor_scalar_mul(
-            woven_direct[:].rearrange("p (c i t) -> p c t i", i=4, t=4),
-            planes_direct.rearrange("p t (c i) -> p c t i", i=4),
-            2.0,
-        )
-        quantize_pair(TURNED, woven_direct[:])
+        def empty(h, b, on_scalar):
+            leave_psum(dx[b][:, h * T : (h + 1) * T], accs[h, b][:], on_scalar)
 
-        for e0, number in BLOCK0:
-            second_product(0, e0, 2, number)
-        for b in range(1, 4):
-            for h in range(2):
-                second_product(b, 4 * h, 4, BLOCK_BANKS[b - 1][h])
+        make_pairs(0)
+        make_pairs(1)
+        make_factor(2)
+        weave_pairs()
+        make_da(0)
+        quantize(OWN)
+        second_product(OWN)
+        make_factor(3)
+        quantize(0)
+        second_product(0)
+        for b in range(4):
+            empty(0, b, True)
+        make_da(2)
+        make_da(3)
+        quantize(2)
+        quantize(3)
+        for b in range(4):
+            second_product(2, [b])
+            second_product(3, [b])
 
         first = [keep.tile([P, T], F32, name="first_%d" % b) for b in range(4)]
+        total = [keep.tile([P, T], F32, name="total_%d" % b) for b in range(4)]
 
         def fetch_first(b, pieces):
             for t0, w in pieces:
-                nc.vector.tensor_copy(first[b][:, t0 : t0 + w], dx[b][:].indirect(pos1_t[:, t0 // 16 : (t0 + w) // 16]))
+                nc.scalar.activation(
+                    first[b][:, t0 : t0 + w], dx[b][:].indirect(pos1_t[:, t0 // 16 : (t0 + w) // 16]), COPY
+                )
 
-        def add_second(b, total, t0, w):
+        def add_second(b, t0, w):
             nc.vector.tensor_tensor(
-                total[:, t0 : t0 + w],
+                total[b][:, t0 : t0 + w],
                 dx[b][:].indirect(pos2_t[:, t0 // 16 : (t0 + w) // 16]),
                 first[b][:, t0 : t0 + w],
                 ADD,
             )
 
-        def add_and_store(b, pieces, tag):
-            total = keep.tile([P, T], F32, name="total_%d" % b, tag=tag, align_bytes=64)
+        def add_and_store(b, pieces):
             for t0, w in pieces:
-                add_second(b, total, t0, w)
-            nc.sync.dma_start(out[b * P : (b + 1) * P, :], total[:])
+                add_second(b, t0, w)
+            nc.sync.dma_start(out[b * P : (b + 1) * P, :], total[b][:])
 
-        fetch_first(0, HALVES)
-        add_and_store(0, HALVES, "total_0")
+        empty(1, 0, False)
+        empty(1, 1, True)
+        empty(1, 2, False)
+        empty(1, 3, False)
+        fetch_first(0, WHOLE)
+        add_and_store(0, WHOLE)
         fetch_first(1, WHOLE)
+        add_and_store(1, WHOLE)
         fetch_first(2, WHOLE)
-        add_and_store(1, WHOLE, "w1_w")
-        add_and_store(2, WHOLE, "total_2")
-        fetch_first(3, HALVES)
-        total_last = keep.tile([P, T], F32, name="total_3", align_bytes=64)
+        add_and_store(2, WHOLE)
+        fetch_first(3, WHOLE)
         for t0, w in TAIL:
-            add_second(3, total_last, t0, w)
-            nc.sync.dma_start(out[3 * P : 4 * P, t0 : t0 + w], total_last[:, t0 : t0 + w])
+            add_second(3, t0, w)
+            nc.sync.dma_start(out[3 * P : 4 * P, t0 : t0 + w], total[3][:, t0 : t0 + w])

@@ -25,7 +25,6 @@ GROUPS = [(0, 2), (2, 2), (4, 3), (7, 1)]
 OWN = 1
 WHOLE = [(0, T)]
 HALVES = [(0, T // 2), (T // 2, T // 2)]
-TAIL = [(0, T // 2), (T // 2, T // 4), (3 * T // 4, T // 4)]
 
 
 def tile_moe_sdb_relu2_kernel(
@@ -52,7 +51,14 @@ def tile_moe_sdb_relu2_kernel(
         first_width = GROUPS[0][1] * C
         gate_first = keep.tile([P, first_width], F32, name="gate_first")
         gate_rest = keep.tile([P, S - first_width], F32, name="gate_rest")
-        a_t = [keep.tile([P, 4, n * C], F32, name="a_%d" % g) for g, (e0, n) in enumerate(GROUPS)]
+        late = keep.tile([P, 16 * C], F32, name="late")
+        late_factor = {2: late[:, 0 : 12 * C], 3: late[:, 12 * C : 16 * C]}
+        a_t = [
+            late[:, 8 * C : 16 * C].rearrange("p (t s) -> p t s", t=4)
+            if g == OWN
+            else keep.tile([P, 4, n * C], F32, name="a_%d" % g)
+            for g, (e0, n) in enumerate(GROUPS)
+        ]
 
         nc.gpsimd.memset(head_s[:].bitcast(I32), 0)
         nc.vector.memset(w1_s[:].rearrange("p e k -> p (e k)").bitcast(I32), 0)
@@ -64,11 +70,11 @@ def tile_moe_sdb_relu2_kernel(
             nc.sync.dma_start(a_t[g][:], a_planes[:, :, e0 * C : (e0 + n) * C])
 
         nc.sync.dma_start(w2_raw[:].bitcast(I32), w2t_words[0].bitcast(I32))
+        nc.sync.dma_start(dy_w[:].bitcast(I32), dy_words[0].rearrange("p t d -> p (t d)").bitcast(I32))
         for r in range(4):
             nc.sync.dma_start(head_s[r:P:32, T : T + H].bitcast(I32), w2t_scales[0, r:16:4, :].bitcast(I32))
         nc.sync.dma_start(gate_first[:], gate[:, 0:first_width])
         load_a(0)
-        nc.sync.dma_start(dy_w[:].bitcast(I32), dy_words[0].rearrange("p t d -> p (t d)").bitcast(I32))
         for r in range(4):
             nc.sync.dma_start(head_s[r:P:32, 0:T].bitcast(I32), dy_scales[0, r:16:4, :].bitcast(I32))
         nc.sync.dma_start(gate_rest[:], gate[:, first_width:S])
@@ -110,7 +116,10 @@ def tile_moe_sdb_relu2_kernel(
 
         def make_factor(g):
             w = GROUPS[g][1] * C
-            factor[g] = keep.tile([P, 4, w], F32, name="factor_%d" % g)
+            if g == 0:
+                factor[g] = keep.tile([P, 4, w], F32, name="factor_0")
+            else:
+                factor[g] = late_factor[g].rearrange("p (t s) -> p t s", t=4)
             nc.vector.scalar_tensor_tensor(
                 factor[g][:], a_t[g][:], 0.0, gate_cols(g).unsqueeze(1).broadcast_to([P, 4, w]), MAX, MULT
             )
@@ -210,15 +219,15 @@ def tile_moe_sdb_relu2_kernel(
             leave_psum(dx[b][:, h * T : (h + 1) * T], accs[h, b][:], on_scalar)
 
         make_pairs(0)
-        make_pairs(1)
         make_factor(2)
-        weave_pairs()
+        make_pairs(1)
         make_da(0)
+        weave_pairs()
+        quantize(0)
+        second_product(0)
         quantize(OWN)
         second_product(OWN)
         make_factor(3)
-        quantize(0)
-        second_product(0)
         for b in range(4):
             empty(0, b, True)
         make_da(2)
@@ -262,6 +271,10 @@ def tile_moe_sdb_relu2_kernel(
         fetch_first(2, WHOLE)
         add_and_store(2, WHOLE)
         fetch_first(3, WHOLE)
-        for t0, w in TAIL:
-            add_second(3, t0, w)
-            nc.sync.dma_start(out[3 * P : 4 * P, t0 : t0 + w], total[3][:, t0 : t0 + w])
+        half = T // 2
+        second = keep.tile([P, half], F32, name="second")
+        nc.scalar.activation(second[:], dx[3][:].indirect(pos2_t[:, half // 16 : T // 16]), COPY)
+        add_second(3, 0, half)
+        nc.sync.dma_start(out[3 * P : 4 * P, 0:half], total[3][:, 0:half])
+        nc.vector.tensor_tensor(total[3][:, half:T], second[:], first[3][:, half:T], ADD)
+        nc.sync.dma_start(out[3 * P : 4 * P, half:T], total[3][:, half:T])

@@ -21,10 +21,11 @@ MAX = mybir.AluOpType.max
 COPY = mybir.ActivationFunctionType.Copy
 RELU = mybir.ActivationFunctionType.Relu
 
-GROUPS = [(0, 2), (2, 2), (4, 3), (7, 1)]
-OWN = 1
-WHOLE = [(0, T)]
-HALVES = [(0, T // 2), (T // 2, T // 2)]
+OWN = (0, 288)
+EARLY = (288, 224)
+LAST = (4 * C, C)
+LONG = (5 * C, 3 * C)
+HALF = S // 2
 
 
 def tile_moe_sdb_relu2_kernel(
@@ -38,6 +39,12 @@ def tile_moe_sdb_relu2_kernel(
         def bank(number):
             return psum.tile([P, T], F32, name="bank_%d" % number, tag="bank_%d" % number)
 
+        def planes(flat):
+            return flat.rearrange("p (t s) -> p t s", t=4)
+
+        def slots(group):
+            return slice(group[0], group[0] + group[1])
+
         offs_t = keep.tile([P, S // 16], U16, name="offs_t")
         pos1_t = keep.tile([P, T // 16], U16, name="pos1_t")
         pos2_t = keep.tile([P, T // 16], U16, name="pos2_t")
@@ -48,40 +55,37 @@ def tile_moe_sdb_relu2_kernel(
         w2_s = keep.tile([P, H], U8, name="w2_s", align_bytes=64)
         w1_w = keep.tile([P, E, 2 * K], U8, name="w1_w", align_bytes=64)
         w1_s = keep.tile([P, E, K], U8, name="w1_s", align_bytes=64)
-        first_width = GROUPS[0][1] * C
-        gate_first = keep.tile([P, first_width], F32, name="gate_first")
-        gate_rest = keep.tile([P, S - first_width], F32, name="gate_rest")
-        late = keep.tile([P, 16 * C], F32, name="late")
-        late_factor = {2: late[:, 0 : 12 * C], 3: late[:, 12 * C : 16 * C]}
-        a_t = [
-            late[:, 8 * C : 16 * C].rearrange("p (t s) -> p t s", t=4)
-            if g == OWN
-            else keep.tile([P, 4, n * C], F32, name="a_%d" % g)
-            for g, (e0, n) in enumerate(GROUPS)
-        ]
+        gate_t = keep.tile([P, S], F32, name="gate_t")
+        a_early = keep.tile([P, 4, EARLY[1]], F32, name="a_early")
+        a_last = keep.tile([P, 4, LAST[1]], F32, name="a_last")
+        a_long = keep.tile([P, 4, LONG[1]], F32, name="a_long")
+        factor_early = keep.tile([P, 4, EARLY[1]], F32, name="factor_early")
+        factor_last = keep.tile([P, 4, LAST[1]], F32, name="factor_last")
+        factor_long = planes(keep.tile([P, 4 * LONG[1]], F32, name="factor_long")[:])
+        a_own = planes(keep.tile([P, 4 * OWN[1]], F32, name="a_own")[:])
 
         nc.gpsimd.memset(head_s[:].bitcast(I32), 0)
         nc.vector.memset(w1_s[:].rearrange("p e k -> p (e k)").bitcast(I32), 0)
 
         a_planes = a.rearrange("(p t) s -> p t s", t=4)
 
-        def load_a(g):
-            e0, n = GROUPS[g]
-            nc.sync.dma_start(a_t[g][:], a_planes[:, :, e0 * C : (e0 + n) * C])
+        def load_gate(s0, s1):
+            nc.sync.dma_start(gate_t[:, s0:s1], gate[:, s0:s1])
 
         nc.sync.dma_start(w2_raw[:].bitcast(I32), w2t_words[0].bitcast(I32))
         nc.sync.dma_start(dy_w[:].bitcast(I32), dy_words[0].rearrange("p t d -> p (t d)").bitcast(I32))
         for r in range(4):
             nc.sync.dma_start(head_s[r:P:32, T : T + H].bitcast(I32), w2t_scales[0, r:16:4, :].bitcast(I32))
-        nc.sync.dma_start(gate_first[:], gate[:, 0:first_width])
-        load_a(0)
+        load_gate(EARLY[0], LONG[0])
+        nc.sync.dma_start(a_early[:], a_planes[:, :, slots(EARLY)])
         for r in range(4):
             nc.sync.dma_start(head_s[r:P:32, 0:T].bitcast(I32), dy_scales[0, r:16:4, :].bitcast(I32))
-        nc.sync.dma_start(gate_rest[:], gate[:, first_width:S])
+        nc.sync.dma_start(a_last[:], a_planes[:, :, slots(LAST)])
+        load_gate(0, EARLY[0])
         nc.sync.dma_start(offs_t[:], offs)
-        load_a(1)
-        load_a(2)
-        load_a(3)
+        load_gate(LONG[0], S)
+        nc.sync.dma_start(a_long[:], a_planes[:, :, slots(LONG)])
+        nc.sync.dma_start(a_own, a_planes[:, :, slots(OWN)])
         nc.sync.dma_start(w1_w[:].bitcast(I32), w1t_words.rearrange("e o p n -> p (e o) n").bitcast(I32))
         for r in range(4):
             nc.sync.dma_start(
@@ -100,29 +104,9 @@ def tile_moe_sdb_relu2_kernel(
             head_s[:, T : T + H].rearrange("p (m t) -> p t m", t=4),
         )
 
-        def gate_cols(g):
-            e0, n = GROUPS[g]
-            if g == 0:
-                return gate_first[:]
-            return gate_rest[:, e0 * C - first_width : (e0 + n) * C - first_width]
-
-        def group_offs(g):
-            e0, n = GROUPS[g]
-            return offs_t[:, e0 * C // 16 : (e0 + n) * C // 16]
-
-        own_width = GROUPS[OWN][1] * C
-
-        factor = {}
-
-        def make_factor(g):
-            w = GROUPS[g][1] * C
-            if g == 0:
-                factor[g] = keep.tile([P, 4, w], F32, name="factor_0")
-            else:
-                factor[g] = late_factor[g].rearrange("p (t s) -> p t s", t=4)
-            nc.vector.scalar_tensor_tensor(
-                factor[g][:], a_t[g][:], 0.0, gate_cols(g).unsqueeze(1).broadcast_to([P, 4, w]), MAX, MULT
-            )
+        def make_factor(factor, a_group, group):
+            gate_cols = gate_t[:, slots(group)].unsqueeze(1).broadcast_to([P, 4, group[1]])
+            nc.vector.scalar_tensor_tensor(factor, a_group, 0.0, gate_cols, MAX, MULT)
 
         dc = [keep.tile([P, T], F32, name="dc_%d" % t) for t in range(4)]
 
@@ -139,45 +123,61 @@ def tile_moe_sdb_relu2_kernel(
             )
             nc.scalar.activation(dc[t][:, n0 : n0 + w], acc[:, 0:w], COPY, scale=2.0)
 
-        def leave_psum(dst, src, on_scalar):
-            if on_scalar:
-                nc.scalar.activation(dst, src, COPY)
-            else:
-                nc.vector.tensor_copy(dst, src)
-
-        make_factor(0)
+        make_factor(factor_early[:], a_early[:], EARLY)
+        make_factor(factor_last[:], a_last[:], LAST)
         first_product(0, 0, T // 2, 0)
         first_product(0, T // 2, T // 2, 4)
         for t in range(1, 4):
             first_product(t, 0, T, t)
 
-        picked = [keep.tile([P, 4, n * C], F32, name="picked_%d" % g) for g, (e0, n) in enumerate(GROUPS)]
-        for g in range(len(GROUPS)):
-            for t in range(4):
-                window = dc[t][:].indirect(group_offs(g))
-                if g == OWN:
-                    nc.vector.tensor_tensor(picked[g][:, t, :], window, gate_cols(g), MULT)
-                else:
-                    nc.scalar.activation(picked[g][:, t, :], window, COPY)
+        def window(t, group):
+            return dc[t][:].indirect(offs_t[:, group[0] // 16 : (group[0] + group[1]) // 16])
 
-        da = [keep.tile([P, 4 * n * C], BF16, name="da_%d" % g, align_bytes=64) for g, (e0, n) in enumerate(GROUPS)]
+        picked = {}
+
+        spent = keep.tile([P, 4 * LAST[1] + 2 * LONG[1]], F32, name="spent", tag="spent", align_bytes=64)
+        pairs = spent[:, 4 * LAST[1] - OWN[1] : 4 * LAST[1] + OWN[1]].bitcast(BF16)
+        pairs = pairs.rearrange("p (u s d) -> p u s d", u=2, d=2)
+
+        def gather(group):
+            if group == LAST:
+                picked[group] = planes(spent[:, 0 : 4 * LAST[1]])
+            else:
+                picked[group] = keep.tile([P, 4, group[1]], F32, name="picked_%d" % group[0])
+            for t in range(4):
+                if group == OWN:
+                    nc.vector.tensor_tensor(picked[group][:, t, :], window(t, group), gate_t[:, slots(group)], MULT)
+                else:
+                    nc.scalar.activation(picked[group][:, t, :], window(t, group), COPY)
+
+        for group in (EARLY, OWN, LONG):
+            gather(group)
+
+        da_low = keep.tile([P, 4 * HALF], BF16, name="da_low", align_bytes=64)
+        da_last = keep.tile([P, 4 * LAST[1]], BF16, name="da_last", align_bytes=64)
+        da_long = spent[:, 4 * LAST[1] : 4 * LAST[1] + 2 * LONG[1]].bitcast(BF16)
         codes = keep.tile([P, S], U32, name="codes", align_bytes=64)
         scales = keep.tile([P, S], U8, name="scales", align_bytes=64)
 
-        def make_da(g):
+        def woven(group):
+            if group == LAST:
+                return da_last[:]
+            if group == LONG:
+                return da_long[:]
+            return da_low[:, 4 * group[0] : 4 * (group[0] + group[1])]
+
+        def make_da(group, factor):
             nc.vector.tensor_tensor(
-                da[g][:].rearrange("p (c i t) -> p c t i", i=2, t=4),
-                picked[g][:].rearrange("p t (c i) -> p c t i", i=2),
-                factor[g][:].rearrange("p t (c i) -> p c t i", i=2),
+                woven(group).rearrange("p (c i t) -> p c t i", i=2, t=4),
+                picked[group][:].rearrange("p t (c i) -> p c t i", i=2),
+                factor.rearrange("p t (c i) -> p c t i", i=2),
                 MULT,
             )
-
-        pairs = keep.tile([P, 2, own_width, 2], BF16, name="pairs")
 
         def make_pairs(u):
             nc.vector.scalar_tensor_tensor(
                 pairs[:, u, :, :],
-                a_t[OWN][:, 2 * u : 2 * u + 2, :].rearrange("p d s -> p s d"),
+                a_own[:, 2 * u : 2 * u + 2, :].rearrange("p d s -> p s d"),
                 0.0,
                 picked[OWN][:, 2 * u : 2 * u + 2, :].rearrange("p d s -> p s d"),
                 MAX,
@@ -186,20 +186,20 @@ def tile_moe_sdb_relu2_kernel(
 
         def weave_pairs():
             nc.vector.tensor_copy(
-                da[OWN][:].bitcast(F32).rearrange("p (s u) -> p s u", u=2),
+                woven(OWN).bitcast(F32).rearrange("p (s u) -> p s u", u=2),
                 pairs[:].rearrange("p u s d -> p u (s d)").bitcast(F32).rearrange("p u s -> p s u"),
             )
 
-        def quantize(g):
-            e0, n = GROUPS[g]
-            cols = slice(e0 * C, (e0 + n) * C)
-            nc.vector.quantize_mx(out=codes[:, cols].bitcast(FP8X4), scales=scales[:, cols], in_=da[g][:])
+        def quantize(e0, n):
+            group = (e0 * C, n * C)
+            nc.vector.quantize_mx(
+                out=codes[:, slots(group)].bitcast(FP8X4), scales=scales[:, slots(group)], in_=woven(group)
+            )
 
-        dx = [keep.tile([P, S], F32, name="dx_%d" % b) for b in range(4)]
+        dx = [keep.tile([P, S], F32, name="dx_%d" % b) for b in range(3)]
         accs = {}
 
-        def second_product(g, blocks=range(4)):
-            e0, n = GROUPS[g]
+        def second_product(e0, n, blocks):
             for b in blocks:
                 key = (e0 // 4, b)
                 if key not in accs:
@@ -216,65 +216,62 @@ def tile_moe_sdb_relu2_kernel(
                     )
 
         def empty(h, b, on_scalar):
-            leave_psum(dx[b][:, h * T : (h + 1) * T], accs[h, b][:], on_scalar)
+            dst = dx[b][:, h * HALF : (h + 1) * HALF]
+            if on_scalar:
+                nc.scalar.activation(dst, accs[h, b][:], COPY)
+            else:
+                nc.vector.tensor_copy(dst, accs[h, b][:])
 
+        make_factor(factor_long, a_long[:], LONG)
         make_pairs(0)
-        make_factor(2)
         make_pairs(1)
-        make_da(0)
+        make_da(EARLY, factor_early[:])
         weave_pairs()
-        quantize(0)
-        second_product(0)
-        quantize(OWN)
-        second_product(OWN)
-        make_factor(3)
+        gather(LAST)
+        quantize(3, 1)
+        quantize(0, 3)
         for b in range(4):
-            empty(0, b, True)
-        make_da(2)
-        make_da(3)
-        quantize(2)
-        quantize(3)
+            second_product(3, 1, [b])
+            second_product(0, 3, [b])
+            if b < 3:
+                empty(0, b, True)
+        make_da(LONG, factor_long)
+        make_da(LAST, factor_last[:])
+        quantize(5, 3)
+        quantize(4, 1)
+        dx.append(keep.tile([P, S], F32, name="dx_3", tag="spent", align_bytes=64))
+        empty(0, 3, False)
+        second_product(5, 3, [0])
         for b in range(4):
-            second_product(2, [b])
-            second_product(3, [b])
+            second_product(4, 1, [b])
+            if b:
+                second_product(5, 3, [b])
 
         first = [keep.tile([P, T], F32, name="first_%d" % b) for b in range(4)]
         total = [keep.tile([P, T], F32, name="total_%d" % b) for b in range(4)]
 
-        def fetch_first(b, pieces):
-            for t0, w in pieces:
-                nc.scalar.activation(
-                    first[b][:, t0 : t0 + w], dx[b][:].indirect(pos1_t[:, t0 // 16 : (t0 + w) // 16]), COPY
-                )
+        def fetch(dst, b, pos_t, t0, t1):
+            nc.scalar.activation(dst, dx[b][:].indirect(pos_t[:, t0 // 16 : t1 // 16]), COPY)
 
-        def add_second(b, t0, w):
+        def add_second(b, t0, t1):
             nc.vector.tensor_tensor(
-                total[b][:, t0 : t0 + w],
-                dx[b][:].indirect(pos2_t[:, t0 // 16 : (t0 + w) // 16]),
-                first[b][:, t0 : t0 + w],
-                ADD,
+                total[b][:, t0:t1], dx[b][:].indirect(pos2_t[:, t0 // 16 : t1 // 16]), first[b][:, t0:t1], ADD
             )
 
-        def add_and_store(b, pieces):
-            for t0, w in pieces:
-                add_second(b, t0, w)
-            nc.sync.dma_start(out[b * P : (b + 1) * P, :], total[b][:])
+        def store(b, t0, t1):
+            nc.sync.dma_start(out[b * P : (b + 1) * P, t0:t1], total[b][:, t0:t1])
 
-        empty(1, 0, False)
-        empty(1, 1, True)
-        empty(1, 2, False)
-        empty(1, 3, False)
-        fetch_first(0, WHOLE)
-        add_and_store(0, WHOLE)
-        fetch_first(1, WHOLE)
-        add_and_store(1, WHOLE)
-        fetch_first(2, WHOLE)
-        add_and_store(2, WHOLE)
-        fetch_first(3, WHOLE)
-        half = T // 2
-        second = keep.tile([P, half], F32, name="second")
-        nc.scalar.activation(second[:], dx[3][:].indirect(pos2_t[:, half // 16 : T // 16]), COPY)
-        add_second(3, 0, half)
-        nc.sync.dma_start(out[3 * P : 4 * P, 0:half], total[3][:, 0:half])
-        nc.vector.tensor_tensor(total[3][:, half:T], second[:], first[3][:, half:T], ADD)
-        nc.sync.dma_start(out[3 * P : 4 * P, half:T], total[3][:, half:T])
+        for b in range(4):
+            empty(1, b, b == 0)
+        for b in range(3):
+            fetch(first[b][:], b, pos1_t, 0, T)
+            add_second(b, 0, T)
+            store(b, 0, T)
+        cut = 256
+        second = keep.tile([P, T - cut], F32, name="second")
+        fetch(first[3][:], 3, pos1_t, 0, T)
+        fetch(second[:], 3, pos2_t, cut, T)
+        add_second(3, 0, cut)
+        store(3, 0, cut)
+        nc.vector.tensor_tensor(total[3][:, cut:T], second[:], first[3][:, cut:T], ADD)
+        store(3, cut, T)

@@ -64,7 +64,7 @@ def tile_moe_sdb_relu2_kernel(
         factor_long = planes(keep.tile([P, 4 * LONG[1]], F32, name="factor_long")[:])
         a_own = planes(keep.tile([P, 4 * OWN[1]], F32, name="a_own")[:])
 
-        nc.gpsimd.memset(head_s[:].bitcast(I32), 0)
+        nc.vector.memset(head_s[:].bitcast(I32), 0)
         nc.vector.memset(w1_s[:].rearrange("p e k -> p (e k)").bitcast(I32), 0)
 
         a_planes = a.rearrange("(p t) s -> p t s", t=4)

@@ -19,13 +19,13 @@ MULT = mybir.AluOpType.mult
 ADD = mybir.AluOpType.add
 MAX = mybir.AluOpType.max
 COPY = mybir.ActivationFunctionType.Copy
-RELU = mybir.ActivationFunctionType.Relu
 
-OWN = (0, 288)
-EARLY = (288, 224)
+OWN = (0, 2 * C)
+EARLY = (2 * C, 2 * C)
 LAST = (4 * C, C)
 LONG = (5 * C, 3 * C)
 HALF = S // 2
+UPPER = (HALF, HALF)
 
 
 def tile_moe_sdb_relu2_kernel(
@@ -49,43 +49,42 @@ def tile_moe_sdb_relu2_kernel(
         pos1_t = keep.tile([P, T // 16], U16, name="pos1_t")
         pos2_t = keep.tile([P, T // 16], U16, name="pos2_t")
         dy_w = keep.tile([P, T], U32, name="dy_w", align_bytes=64)
-        head_s = keep.tile([P, T + H], U8, name="head_s", align_bytes=64)
+        dy_rows = keep.tile([4, 4, T], U8, name="dy_rows", align_bytes=64)
+        dy_s = keep.tile([P, T], U8, name="dy_s", align_bytes=64)
         w2_raw = keep.tile([P, 2 * H], U8, name="w2_raw", align_bytes=64)
         w2_w = keep.tile([P, 2 * H], U8, name="w2_w", align_bytes=64)
+        w2_s_raw = keep.tile([P, H], U8, name="w2_s_raw", align_bytes=64)
         w2_s = keep.tile([P, H], U8, name="w2_s", align_bytes=64)
         w1_w = keep.tile([P, E, 2 * K], U8, name="w1_w", align_bytes=64)
         w1_s = keep.tile([P, E, K], U8, name="w1_s", align_bytes=64)
         gate_t = keep.tile([P, S], F32, name="gate_t")
         a_early = keep.tile([P, 4, EARLY[1]], F32, name="a_early")
-        a_last = keep.tile([P, 4, LAST[1]], F32, name="a_last")
-        a_long = keep.tile([P, 4, LONG[1]], F32, name="a_long")
+        a_upper = keep.tile([P, 4, HALF], F32, name="a_upper")
+        a_own = keep.tile([P, 4, OWN[1]], F32, name="a_own")
         factor_early = keep.tile([P, 4, EARLY[1]], F32, name="factor_early")
-        factor_last = keep.tile([P, 4, LAST[1]], F32, name="factor_last")
-        factor_long = planes(keep.tile([P, 4 * LONG[1]], F32, name="factor_long")[:])
-        a_own = planes(keep.tile([P, 4 * OWN[1]], F32, name="a_own")[:])
+        factor_upper = keep.tile([P, 4, HALF], F32, name="factor_upper")
 
-        nc.vector.memset(head_s[:].bitcast(I32), 0)
+        nc.vector.memset(w2_s_raw[:].bitcast(I32), 0)
+        nc.vector.memset(dy_s[:].bitcast(I32), 0)
         nc.vector.memset(w1_s[:].rearrange("p e k -> p (e k)").bitcast(I32), 0)
 
         a_planes = a.rearrange("(p t) s -> p t s", t=4)
 
-        def load_gate(s0, s1):
-            nc.sync.dma_start(gate_t[:, s0:s1], gate[:, s0:s1])
+        def load_gate(group):
+            nc.sync.dma_start(gate_t[:, slots(group)], gate[:, slots(group)])
 
+        nc.sync.dma_start(dy_rows[:].bitcast(I32), dy_scales[0].rearrange("(q r) t -> r q t", r=4).bitcast(I32))
         nc.sync.dma_start(w2_raw[:].bitcast(I32), w2t_words[0].bitcast(I32))
         nc.sync.dma_start(dy_w[:].bitcast(I32), dy_words[0].rearrange("p t d -> p (t d)").bitcast(I32))
         for r in range(4):
-            nc.sync.dma_start(head_s[r:P:32, T : T + H].bitcast(I32), w2t_scales[0, r:16:4, :].bitcast(I32))
-        load_gate(EARLY[0], LONG[0])
+            nc.sync.dma_start(w2_s_raw[r:P:32, :].bitcast(I32), w2t_scales[0, r:16:4, :].bitcast(I32))
         nc.sync.dma_start(a_early[:], a_planes[:, :, slots(EARLY)])
-        for r in range(4):
-            nc.sync.dma_start(head_s[r:P:32, 0:T].bitcast(I32), dy_scales[0, r:16:4, :].bitcast(I32))
-        nc.sync.dma_start(a_last[:], a_planes[:, :, slots(LAST)])
-        load_gate(0, EARLY[0])
+        load_gate(EARLY)
         nc.sync.dma_start(offs_t[:], offs)
-        load_gate(LONG[0], S)
-        nc.sync.dma_start(a_long[:], a_planes[:, :, slots(LONG)])
-        nc.sync.dma_start(a_own, a_planes[:, :, slots(OWN)])
+        load_gate(OWN)
+        nc.sync.dma_start(a_own[:], a_planes[:, :, slots(OWN)])
+        load_gate(UPPER)
+        nc.sync.dma_start(a_upper[:], a_planes[:, :, slots(UPPER)])
         nc.sync.dma_start(w1_w[:].bitcast(I32), w1t_words.rearrange("e o p n -> p (e o) n").bitcast(I32))
         for r in range(4):
             nc.sync.dma_start(
@@ -95,13 +94,15 @@ def tile_moe_sdb_relu2_kernel(
         nc.sync.dma_start(pos1_t[:], pos1)
         nc.sync.dma_start(pos2_t[:], pos2)
 
+        for q in range(4):
+            nc.vector.tensor_copy(dy_s[32 * q : 32 * q + 4, :].bitcast(I32), dy_rows[:, q, :].bitcast(I32))
         nc.vector.tensor_copy(
             w2_w[:].bitcast(U16).rearrange("p (t m) -> p t m", t=4),
             w2_raw[:].bitcast(U16).rearrange("p (m t) -> p t m", t=4),
         )
         nc.vector.tensor_copy(
             w2_s[:].rearrange("p (t m) -> p t m", t=4),
-            head_s[:, T : T + H].rearrange("p (m t) -> p t m", t=4),
+            w2_s_raw[:].rearrange("p (m t) -> p t m", t=4),
         )
 
         def make_factor(factor, a_group, group):
@@ -117,14 +118,13 @@ def tile_moe_sdb_relu2_kernel(
                 lhsT=w2_w[:, 2 * P * t : 2 * P * (t + 1)].bitcast(FP4X4),
                 lhsT_scale=w2_s[:, P * t : P * (t + 1)],
                 rhs=dy_w[:, n0 : n0 + w].bitcast(FP8X4),
-                rhs_scale=head_s[:, n0 : n0 + w],
+                rhs_scale=dy_s[:, n0 : n0 + w],
                 start=True,
                 stop=True,
             )
             nc.scalar.activation(dc[t][:, n0 : n0 + w], acc[:, 0:w], COPY, scale=2.0)
 
         make_factor(factor_early[:], a_early[:], EARLY)
-        make_factor(factor_last[:], a_last[:], LAST)
         first_product(0, 0, T // 2, 0)
         first_product(0, T // 2, T // 2, 4)
         for t in range(1, 4):
@@ -190,8 +190,7 @@ def tile_moe_sdb_relu2_kernel(
                 pairs[:].rearrange("p u s d -> p u (s d)").bitcast(F32).rearrange("p u s -> p s u"),
             )
 
-        def quantize(e0, n):
-            group = (e0 * C, n * C)
+        def quantize(group):
             nc.vector.quantize_mx(
                 out=codes[:, slots(group)].bitcast(FP8X4), scales=scales[:, slots(group)], in_=woven(group)
             )
@@ -199,21 +198,21 @@ def tile_moe_sdb_relu2_kernel(
         dx = [keep.tile([P, S], F32, name="dx_%d" % b) for b in range(3)]
         accs = {}
 
-        def second_product(e0, n, blocks):
-            for b in blocks:
-                key = (e0 // 4, b)
-                if key not in accs:
-                    accs[key] = bank(4 * (e0 // 4) + b)
-                for e in range(e0, e0 + n):
-                    nc.tensor.matmul_mx(
-                        out=accs[key][:, (e % 4) * C : (e % 4 + 1) * C],
-                        lhsT=w1_w[:, e, 2 * P * b : 2 * P * (b + 1)].bitcast(FP4X4),
-                        lhsT_scale=w1_s[:, e, P * b : P * (b + 1)],
-                        rhs=codes[:, e * C : (e + 1) * C].bitcast(FP8X4),
-                        rhs_scale=scales[:, e * C : (e + 1) * C],
-                        start=True,
-                        stop=True,
-                    )
+        def second_product(group, b):
+            e0 = group[0] // C
+            key = (e0 // 4, b)
+            if key not in accs:
+                accs[key] = bank(4 * (e0 // 4) + b)
+            for e in range(e0, e0 + group[1] // C):
+                nc.tensor.matmul_mx(
+                    out=accs[key][:, (e % 4) * C : (e % 4 + 1) * C],
+                    lhsT=w1_w[:, e, 2 * P * b : 2 * P * (b + 1)].bitcast(FP4X4),
+                    lhsT_scale=w1_s[:, e, P * b : P * (b + 1)],
+                    rhs=codes[:, e * C : (e + 1) * C].bitcast(FP8X4),
+                    rhs_scale=scales[:, e * C : (e + 1) * C],
+                    start=True,
+                    stop=True,
+                )
 
         def empty(h, b, on_scalar):
             dst = dx[b][:, h * HALF : (h + 1) * HALF]
@@ -222,30 +221,33 @@ def tile_moe_sdb_relu2_kernel(
             else:
                 nc.vector.tensor_copy(dst, accs[h, b][:])
 
-        make_factor(factor_long, a_long[:], LONG)
+        def upper_factor(group):
+            return factor_upper[:, :, group[0] - HALF : group[0] - HALF + group[1]]
+
         make_pairs(0)
         make_pairs(1)
+        make_factor(factor_upper[:], a_upper[:], UPPER)
         make_da(EARLY, factor_early[:])
         weave_pairs()
         gather(LAST)
-        quantize(3, 1)
-        quantize(0, 3)
+        quantize(EARLY)
+        quantize(OWN)
         for b in range(4):
-            second_product(3, 1, [b])
-            second_product(0, 3, [b])
+            second_product(EARLY, b)
+            second_product(OWN, b)
             if b < 3:
                 empty(0, b, True)
-        make_da(LONG, factor_long)
-        make_da(LAST, factor_last[:])
-        quantize(5, 3)
-        quantize(4, 1)
+        make_da(LONG, upper_factor(LONG))
+        make_da(LAST, upper_factor(LAST))
+        quantize(LONG)
+        quantize(LAST)
         dx.append(keep.tile([P, S], F32, name="dx_3", tag="spent", align_bytes=64))
         empty(0, 3, False)
-        second_product(5, 3, [0])
+        second_product(LONG, 0)
         for b in range(4):
-            second_product(4, 1, [b])
+            second_product(LAST, b)
             if b:
-                second_product(5, 3, [b])
+                second_product(LONG, b)
 
         first = [keep.tile([P, T], F32, name="first_%d" % b) for b in range(4)]
         total = [keep.tile([P, T], F32, name="total_%d" % b) for b in range(4)]

@@ -26,6 +26,8 @@ LAST = (4 * C, C)
 LONG = (5 * C, 3 * C)
 HALF = S // 2
 UPPER = (HALF, HALF)
+THIRD = (HALF, 2 * C)
+FOURTH = (6 * C, 2 * C)
 
 
 def tile_moe_sdb_relu2_kernel(
@@ -59,7 +61,8 @@ def tile_moe_sdb_relu2_kernel(
         w1_s = keep.tile([P, E, K], U8, name="w1_s", align_bytes=64)
         gate_t = keep.tile([P, S], F32, name="gate_t")
         a_early = keep.tile([P, 4, EARLY[1]], F32, name="a_early")
-        a_upper = keep.tile([P, 4, HALF], F32, name="a_upper")
+        a_third = keep.tile([P, 4, THIRD[1]], F32, name="a_third")
+        a_fourth = keep.tile([P, 4, FOURTH[1]], F32, name="a_fourth")
         a_own = keep.tile([P, 4, OWN[1]], F32, name="a_own")
         factor_early = keep.tile([P, 4, EARLY[1]], F32, name="factor_early")
         factor_upper = keep.tile([P, 4, HALF], F32, name="factor_upper")
@@ -84,13 +87,16 @@ def tile_moe_sdb_relu2_kernel(
         load_gate(OWN)
         nc.sync.dma_start(a_own[:], a_planes[:, :, slots(OWN)])
         load_gate(UPPER)
-        nc.sync.dma_start(a_upper[:], a_planes[:, :, slots(UPPER)])
-        nc.sync.dma_start(w1_w[:].bitcast(I32), w1t_words.rearrange("e o p n -> p (e o) n").bitcast(I32))
+        nc.sync.dma_start(a_third[:], a_planes[:, :, slots(THIRD)])
+        nc.sync.dma_start(a_fourth[:], a_planes[:, :, slots(FOURTH)])
+        w1_rows = w1t_words.rearrange("e o p n -> p (e o) n")
+        nc.sync.dma_start(w1_w[:, 0:4, :].bitcast(I32), w1_rows[:, 0:4, :].bitcast(I32))
         for r in range(4):
             nc.sync.dma_start(
                 w1_s[r:P:32, :, :].bitcast(I32),
                 w1t_scales[:, 0, r:16:4, :].rearrange("e q k -> q e k").bitcast(I32),
             )
+        nc.sync.dma_start(w1_w[:, 4:8, :].bitcast(I32), w1_rows[:, 4:8, :].bitcast(I32))
         nc.sync.dma_start(pos1_t[:], pos1)
         nc.sync.dma_start(pos2_t[:], pos2)
 
@@ -226,10 +232,11 @@ def tile_moe_sdb_relu2_kernel(
 
         make_pairs(0)
         make_pairs(1)
-        make_factor(factor_upper[:], a_upper[:], UPPER)
+        make_factor(upper_factor(THIRD), a_third[:], THIRD)
         make_da(EARLY, factor_early[:])
         weave_pairs()
         gather(LAST)
+        make_factor(upper_factor(FOURTH), a_fourth[:], FOURTH)
         quantize(EARLY)
         quantize(OWN)
         for b in range(4):

@@ -50,22 +50,28 @@ def tile_moe_sdb_relu2_kernel(
         offs_t = keep.tile([P, S // 16], U16, name="offs_t")
         pos1_t = keep.tile([P, T // 16], U16, name="pos1_t")
         pos2_t = keep.tile([P, T // 16], U16, name="pos2_t")
-        dy_w = keep.tile([P, T], U32, name="dy_w", align_bytes=64)
+        dy_w = keep.tile([P, T], U32, name="dy_w", tag="dy_w", align_bytes=64)
         dy_rows = keep.tile([4, 4, T], U8, name="dy_rows", align_bytes=64)
         dy_s = keep.tile([P, T], U8, name="dy_s", align_bytes=64)
         w2_raw = keep.tile([P, 2 * H], U8, name="w2_raw", align_bytes=64)
-        w2_w = keep.tile([P, 2 * H], U8, name="w2_w", align_bytes=64)
+        w2_w = keep.tile([P, 2 * H], U8, name="w2_w", tag="w2_w", align_bytes=64)
         w2_s_raw = keep.tile([P, H], U8, name="w2_s_raw", align_bytes=64)
-        w2_s = keep.tile([P, H], U8, name="w2_s", align_bytes=64)
+        w2_s = keep.tile([P, H], U8, name="w2_s", tag="w2_s", align_bytes=64)
         w1_w = keep.tile([P, E, 2 * K], U8, name="w1_w", align_bytes=64)
         w1_s = keep.tile([P, E, K], U8, name="w1_s", align_bytes=64)
-        gate_t = keep.tile([P, S], F32, name="gate_t")
-        a_early = keep.tile([P, 4, EARLY[1]], F32, name="a_early")
-        a_third = keep.tile([P, 4, THIRD[1]], F32, name="a_third")
+        gate_t = keep.tile([P, S - OWN[1]], F32, name="gate_t")
+        a_early = [keep.tile([P, 2, EARLY[1]], F32, name="a_early_%d" % u) for u in range(2)]
+        a_third_flat = keep.tile([P, 4 * THIRD[1]], F32, name="a_third", align_bytes=64)
+        a_third = planes(a_third_flat[:])
         a_fourth = keep.tile([P, 4, FOURTH[1]], F32, name="a_fourth")
-        a_own = keep.tile([P, 4, OWN[1]], F32, name="a_own")
-        factor_early = keep.tile([P, 4, EARLY[1]], F32, name="factor_early")
+        a_own = [keep.tile([P, 2, OWN[1]], F32, name="a_own_%d" % u) for u in range(2)]
         factor_upper = keep.tile([P, 4, HALF], F32, name="factor_upper")
+        factor_early = factor_upper[:, :, THIRD[1] : HALF]
+
+        warm_in = keep.tile([P, 1], F32, name="warm_in")
+        warm_out = keep.tile([P, 1], F32, name="warm_out")
+        nc.gpsimd.memset(warm_in[:], 0.0)
+        nc.scalar.activation(warm_out[:], warm_in[:], COPY)
 
         nc.vector.memset(w2_s_raw[:].bitcast(I32), 0)
         nc.vector.memset(dy_s[:].bitcast(I32), 0)
@@ -73,21 +79,28 @@ def tile_moe_sdb_relu2_kernel(
 
         a_planes = a.rearrange("(p t) s -> p t s", t=4)
 
+        def gate_of(group):
+            if group == OWN:
+                return factor_upper[:, 3, 0 : OWN[1]]
+            return gate_t[:, group[0] - OWN[1] : group[0] - OWN[1] + group[1]]
+
         def load_gate(group):
-            nc.sync.dma_start(gate_t[:, slots(group)], gate[:, slots(group)])
+            nc.sync.dma_start(gate_of(group), gate[:, slots(group)])
 
         nc.sync.dma_start(dy_rows[:].bitcast(I32), dy_scales[0].rearrange("(q r) t -> r q t", r=4).bitcast(I32))
         nc.sync.dma_start(w2_raw[:].bitcast(I32), w2t_words[0].bitcast(I32))
         nc.sync.dma_start(dy_w[:].bitcast(I32), dy_words[0].rearrange("p t d -> p (t d)").bitcast(I32))
         for r in range(4):
             nc.sync.dma_start(w2_s_raw[r:P:32, :].bitcast(I32), w2t_scales[0, r:16:4, :].bitcast(I32))
-        nc.sync.dma_start(a_early[:], a_planes[:, :, slots(EARLY)])
+        nc.sync.dma_start(a_early[0][:], a_planes[:, 0:2, slots(EARLY)])
         load_gate(EARLY)
+        nc.sync.dma_start(a_early[1][:], a_planes[:, 2:4, slots(EARLY)])
         nc.sync.dma_start(offs_t[:], offs)
         load_gate(OWN)
-        nc.sync.dma_start(a_own[:], a_planes[:, :, slots(OWN)])
+        nc.sync.dma_start(a_own[0][:], a_planes[:, 0:2, slots(OWN)])
         load_gate(UPPER)
-        nc.sync.dma_start(a_third[:], a_planes[:, :, slots(THIRD)])
+        nc.sync.dma_start(a_third, a_planes[:, :, slots(THIRD)])
+        nc.sync.dma_start(a_own[1][:], a_planes[:, 2:4, slots(OWN)])
         nc.sync.dma_start(a_fourth[:], a_planes[:, :, slots(FOURTH)])
         w1_rows = w1t_words.rearrange("e o p n -> p (e o) n")
         nc.sync.dma_start(w1_w[:, 0:4, :].bitcast(I32), w1_rows[:, 0:4, :].bitcast(I32))
@@ -102,7 +115,7 @@ def tile_moe_sdb_relu2_kernel(
 
         for q in range(4):
             nc.vector.tensor_copy(dy_s[32 * q : 32 * q + 4, :].bitcast(I32), dy_rows[:, q, :].bitcast(I32))
-        nc.vector.tensor_copy(
+        nc.scalar.copy(
             w2_w[:].bitcast(U16).rearrange("p (t m) -> p t m", t=4),
             w2_raw[:].bitcast(U16).rearrange("p (m t) -> p t m", t=4),
         )
@@ -112,7 +125,7 @@ def tile_moe_sdb_relu2_kernel(
         )
 
         def make_factor(factor, a_group, group):
-            gate_cols = gate_t[:, slots(group)].unsqueeze(1).broadcast_to([P, 4, group[1]])
+            gate_cols = gate_of(group).unsqueeze(1).broadcast_to(list(factor.shape))
             nc.vector.scalar_tensor_tensor(factor, a_group, 0.0, gate_cols, MAX, MULT)
 
         dc = [keep.tile([P, T], F32, name="dc_%d" % t) for t in range(4)]
@@ -130,7 +143,8 @@ def tile_moe_sdb_relu2_kernel(
             )
             nc.scalar.activation(dc[t][:, n0 : n0 + w], acc[:, 0:w], COPY, scale=2.0)
 
-        make_factor(factor_early[:], a_early[:], EARLY)
+        for u in range(2):
+            make_factor(factor_early[:, 2 * u : 2 * u + 2, :], a_early[u][:], EARLY)
         first_product(0, 0, T // 2, 0)
         first_product(0, T // 2, T // 2, 4)
         for t in range(1, 4):
@@ -140,42 +154,40 @@ def tile_moe_sdb_relu2_kernel(
             return dc[t][:].indirect(offs_t[:, group[0] // 16 : (group[0] + group[1]) // 16])
 
         picked = {}
+        picked_flat = {}
 
-        spent = keep.tile([P, 4 * LAST[1] + 2 * LONG[1]], F32, name="spent", tag="spent", align_bytes=64)
-        pairs = spent[:, 4 * LAST[1] - OWN[1] : 4 * LAST[1] + OWN[1]].bitcast(BF16)
-        pairs = pairs.rearrange("p (u s d) -> p u s d", u=2, d=2)
+        spent = {EARLY: "dy_w", LONG: "w2_w", LAST: "w2_s", OWN: "picked_own"}
 
         def gather(group):
-            if group == LAST:
-                picked[group] = planes(spent[:, 0 : 4 * LAST[1]])
-            else:
-                picked[group] = keep.tile([P, 4, group[1]], F32, name="picked_%d" % group[0])
+            picked_flat[group] = keep.tile(
+                [P, 4 * group[1]], F32, name="picked_%d" % group[0], tag=spent[group], align_bytes=64
+            )
+            picked[group] = planes(picked_flat[group][:])
             for t in range(4):
                 if group == OWN:
-                    nc.vector.tensor_tensor(picked[group][:, t, :], window(t, group), gate_t[:, slots(group)], MULT)
+                    nc.vector.tensor_tensor(picked[group][:, t, :], window(t, group), gate_of(group), MULT)
                 else:
                     nc.scalar.activation(picked[group][:, t, :], window(t, group), COPY)
 
-        for group in (EARLY, OWN, LONG):
+        for group in (EARLY, OWN, LONG, LAST):
             gather(group)
 
-        da_low = keep.tile([P, 4 * HALF], BF16, name="da_low", align_bytes=64)
-        da_last = keep.tile([P, 4 * LAST[1]], BF16, name="da_last", align_bytes=64)
-        da_long = spent[:, 4 * LAST[1] : 4 * LAST[1] + 2 * LONG[1]].bitcast(BF16)
+        pairs_flat = keep.tile([P, 2 * LONG[1]], F32, name="pairs", tag="pairs", align_bytes=64)
+        pairs = pairs_flat[:, 0 : 2 * OWN[1]].bitcast(BF16).rearrange("p (u s d) -> p u s d", u=2, d=2)
+        da_own = keep.tile([P, 4 * OWN[1]], BF16, name="da_own", align_bytes=64)
+        da = {
+            EARLY: a_third_flat[:, 0 : 2 * EARLY[1]].bitcast(BF16),
+            OWN: da_own[:],
+            LONG: pairs_flat[:].bitcast(BF16),
+            LAST: da_own[:, 0 : 4 * LAST[1]],
+        }
         codes = keep.tile([P, S], U32, name="codes", align_bytes=64)
         scales = keep.tile([P, S], U8, name="scales", align_bytes=64)
 
-        def woven(group):
-            if group == LAST:
-                return da_last[:]
-            if group == LONG:
-                return da_long[:]
-            return da_low[:, 4 * group[0] : 4 * (group[0] + group[1])]
-
         def make_da(group, factor):
             nc.vector.tensor_tensor(
-                woven(group).rearrange("p (c i t) -> p c t i", i=2, t=4),
-                picked[group][:].rearrange("p t (c i) -> p c t i", i=2),
+                da[group].rearrange("p (c i t) -> p c t i", i=2, t=4),
+                picked[group].rearrange("p t (c i) -> p c t i", i=2),
                 factor.rearrange("p t (c i) -> p c t i", i=2),
                 MULT,
             )
@@ -183,7 +195,7 @@ def tile_moe_sdb_relu2_kernel(
         def make_pairs(u):
             nc.vector.scalar_tensor_tensor(
                 pairs[:, u, :, :],
-                a_own[:, 2 * u : 2 * u + 2, :].rearrange("p d s -> p s d"),
+                a_own[u][:].rearrange("p d s -> p s d"),
                 0.0,
                 picked[OWN][:, 2 * u : 2 * u + 2, :].rearrange("p d s -> p s d"),
                 MAX,
@@ -192,13 +204,13 @@ def tile_moe_sdb_relu2_kernel(
 
         def weave_pairs():
             nc.vector.tensor_copy(
-                woven(OWN).bitcast(F32).rearrange("p (s u) -> p s u", u=2),
-                pairs[:].rearrange("p u s d -> p u (s d)").bitcast(F32).rearrange("p u s -> p s u"),
+                da[OWN].bitcast(F32).rearrange("p (s u) -> p s u", u=2),
+                pairs.rearrange("p u s d -> p u (s d)").bitcast(F32).rearrange("p u s -> p s u"),
             )
 
         def quantize(group):
             nc.vector.quantize_mx(
-                out=codes[:, slots(group)].bitcast(FP8X4), scales=scales[:, slots(group)], in_=woven(group)
+                out=codes[:, slots(group)].bitcast(FP8X4), scales=scales[:, slots(group)], in_=da[group]
             )
 
         dx = [keep.tile([P, S], F32, name="dx_%d" % b) for b in range(3)]
@@ -231,11 +243,10 @@ def tile_moe_sdb_relu2_kernel(
             return factor_upper[:, :, group[0] - HALF : group[0] - HALF + group[1]]
 
         make_pairs(0)
+        make_factor(upper_factor(THIRD), a_third, THIRD)
         make_pairs(1)
-        make_factor(upper_factor(THIRD), a_third[:], THIRD)
-        make_da(EARLY, factor_early[:])
+        make_da(EARLY, factor_early)
         weave_pairs()
-        gather(LAST)
         make_factor(upper_factor(FOURTH), a_fourth[:], FOURTH)
         quantize(EARLY)
         quantize(OWN)
@@ -248,7 +259,7 @@ def tile_moe_sdb_relu2_kernel(
         make_da(LAST, upper_factor(LAST))
         quantize(LONG)
         quantize(LAST)
-        dx.append(keep.tile([P, S], F32, name="dx_3", tag="spent", align_bytes=64))
+        dx.append(keep.tile([P, S], F32, name="dx_3", tag="pairs", align_bytes=64))
         empty(0, 3, False)
         second_product(LONG, 0)
         for b in range(4):

@@ -26,8 +26,6 @@ LAST = (4 * C, C)
 LONG = (5 * C, 3 * C)
 HALF = S // 2
 UPPER = (HALF, HALF)
-THIRD = (HALF, 2 * C)
-FOURTH = (6 * C, 2 * C)
 
 
 def tile_moe_sdb_relu2_kernel(
@@ -61,12 +59,10 @@ def tile_moe_sdb_relu2_kernel(
         w1_s = keep.tile([P, E, K], U8, name="w1_s", align_bytes=64)
         gate_t = keep.tile([P, S - OWN[1]], F32, name="gate_t")
         a_early = [keep.tile([P, 2, EARLY[1]], F32, name="a_early_%d" % u) for u in range(2)]
-        a_third_flat = keep.tile([P, 4 * THIRD[1]], F32, name="a_third", align_bytes=64)
-        a_third = planes(a_third_flat[:])
-        a_fourth = keep.tile([P, 4, FOURTH[1]], F32, name="a_fourth")
+        a_upper = [keep.tile([P, 2 * HALF], F32, name="a_upper_%d" % u, align_bytes=64) for u in range(2)]
         a_own = [keep.tile([P, 2, OWN[1]], F32, name="a_own_%d" % u) for u in range(2)]
         factor_upper = keep.tile([P, 4, HALF], F32, name="factor_upper")
-        factor_early = factor_upper[:, :, THIRD[1] : HALF]
+        factor_early = planes(factor_upper[:, 2:4, :].rearrange("p t s -> p (t s)"))
 
         warm_in = keep.tile([P, 1], F32, name="warm_in")
         warm_out = keep.tile([P, 1], F32, name="warm_out")
@@ -81,11 +77,17 @@ def tile_moe_sdb_relu2_kernel(
 
         def gate_of(group):
             if group == OWN:
-                return factor_upper[:, 3, 0 : OWN[1]]
+                return factor_upper[:, 1, 0 : OWN[1]]
             return gate_t[:, group[0] - OWN[1] : group[0] - OWN[1] + group[1]]
 
         def load_gate(group):
             nc.sync.dma_start(gate_of(group), gate[:, slots(group)])
+
+        def two_planes(flat):
+            return flat.rearrange("p (t s) -> p t s", t=2)
+
+        def load_upper(u):
+            nc.sync.dma_start(two_planes(a_upper[u][:]), a_planes[:, 2 * u : 2 * u + 2, slots(UPPER)])
 
         nc.sync.dma_start(dy_rows[:].bitcast(I32), dy_scales[0].rearrange("(q r) t -> r q t", r=4).bitcast(I32))
         nc.sync.dma_start(w2_raw[:].bitcast(I32), w2t_words[0].bitcast(I32))
@@ -99,9 +101,9 @@ def tile_moe_sdb_relu2_kernel(
         load_gate(OWN)
         nc.sync.dma_start(a_own[0][:], a_planes[:, 0:2, slots(OWN)])
         load_gate(UPPER)
-        nc.sync.dma_start(a_third, a_planes[:, :, slots(THIRD)])
+        load_upper(0)
         nc.sync.dma_start(a_own[1][:], a_planes[:, 2:4, slots(OWN)])
-        nc.sync.dma_start(a_fourth[:], a_planes[:, :, slots(FOURTH)])
+        load_upper(1)
         w1_rows = w1t_words.rearrange("e o p n -> p (e o) n")
         nc.sync.dma_start(w1_w[:, 0:4, :].bitcast(I32), w1_rows[:, 0:4, :].bitcast(I32))
         for r in range(4):
@@ -113,7 +115,8 @@ def tile_moe_sdb_relu2_kernel(
         nc.sync.dma_start(pos1_t[:], pos1)
         nc.sync.dma_start(pos2_t[:], pos2)
 
-        for q in range(4):
+        nc.scalar.copy(dy_s[0:4, :].bitcast(U32), dy_rows[:, 0, :].bitcast(U32))
+        for q in range(1, 4):
             nc.vector.tensor_copy(dy_s[32 * q : 32 * q + 4, :].bitcast(I32), dy_rows[:, q, :].bitcast(I32))
         nc.scalar.copy(
             w2_w[:].bitcast(U16).rearrange("p (t m) -> p t m", t=4),
@@ -176,7 +179,7 @@ def tile_moe_sdb_relu2_kernel(
         pairs = pairs_flat[:, 0 : 2 * OWN[1]].bitcast(BF16).rearrange("p (u s d) -> p u s d", u=2, d=2)
         da_own = keep.tile([P, 4 * OWN[1]], BF16, name="da_own", align_bytes=64)
         da = {
-            EARLY: a_third_flat[:, 0 : 2 * EARLY[1]].bitcast(BF16),
+            EARLY: a_upper[0][:, 0 : 2 * EARLY[1]].bitcast(BF16),
             OWN: da_own[:],
             LONG: pairs_flat[:].bitcast(BF16),
             LAST: da_own[:, 0 : 4 * LAST[1]],
@@ -243,11 +246,11 @@ def tile_moe_sdb_relu2_kernel(
             return factor_upper[:, :, group[0] - HALF : group[0] - HALF + group[1]]
 
         make_pairs(0)
-        make_factor(upper_factor(THIRD), a_third, THIRD)
+        make_factor(factor_upper[:, 0:2, :], two_planes(a_upper[0][:]), UPPER)
         make_pairs(1)
         make_da(EARLY, factor_early)
         weave_pairs()
-        make_factor(upper_factor(FOURTH), a_fourth[:], FOURTH)
+        make_factor(factor_upper[:, 2:4, :], two_planes(a_upper[1][:]), UPPER)
         quantize(EARLY)
         quantize(OWN)
         for b in range(4):

@@ -55,7 +55,7 @@ def tile_moe_sdb_relu2_kernel(
         w2_w = keep.tile([P, 2 * H], U8, name="w2_w", tag="w2_w", align_bytes=64)
         w2_s_raw = keep.tile([P, H], U8, name="w2_s_raw", align_bytes=64)
         w2_s = keep.tile([P, H], U8, name="w2_s", tag="w2_s", align_bytes=64)
-        w1_w = keep.tile([P, E, 2 * K], U8, name="w1_w", align_bytes=64)
+        w1_w = [keep.tile([P, E // 2, 2 * K], U8, name="w1_low", align_bytes=64)]
         w1_s = keep.tile([P, E, K], U8, name="w1_s", align_bytes=64)
         gate_t = keep.tile([P, S - OWN[1]], F32, name="gate_t")
         a_early = [keep.tile([P, 2, EARLY[1]], F32, name="a_early_%d" % u) for u in range(2)]
@@ -105,13 +105,12 @@ def tile_moe_sdb_relu2_kernel(
         nc.sync.dma_start(a_own[1][:], a_planes[:, 2:4, slots(OWN)])
         load_upper(1)
         w1_rows = w1t_words.rearrange("e o p n -> p (e o) n")
-        nc.sync.dma_start(w1_w[:, 0:4, :].bitcast(I32), w1_rows[:, 0:4, :].bitcast(I32))
+        nc.sync.dma_start(w1_w[0][:].bitcast(I32), w1_rows[:, 0:4, :].bitcast(I32))
         for r in range(4):
             nc.sync.dma_start(
                 w1_s[r:P:32, :, :].bitcast(I32),
                 w1t_scales[:, 0, r:16:4, :].rearrange("e q k -> q e k").bitcast(I32),
             )
-        nc.sync.dma_start(w1_w[:, 4:8, :].bitcast(I32), w1_rows[:, 4:8, :].bitcast(I32))
         nc.sync.dma_start(pos1_t[:], pos1)
         nc.sync.dma_start(pos2_t[:], pos2)
 
@@ -227,7 +226,7 @@ def tile_moe_sdb_relu2_kernel(
             for e in range(e0, e0 + group[1] // C):
                 nc.tensor.matmul_mx(
                     out=accs[key][:, (e % 4) * C : (e % 4 + 1) * C],
-                    lhsT=w1_w[:, e, 2 * P * b : 2 * P * (b + 1)].bitcast(FP4X4),
+                    lhsT=w1_w[e // 4][:, e % 4, 2 * P * b : 2 * P * (b + 1)].bitcast(FP4X4),
                     lhsT_scale=w1_s[:, e, P * b : P * (b + 1)],
                     rhs=codes[:, e * C : (e + 1) * C].bitcast(FP8X4),
                     rhs_scale=scales[:, e * C : (e + 1) * C],
@@ -249,6 +248,8 @@ def tile_moe_sdb_relu2_kernel(
         make_factor(factor_upper[:, 0:2, :], two_planes(a_upper[0][:]), UPPER)
         make_pairs(1)
         make_da(EARLY, factor_early)
+        w1_w.append(keep.tile([P, E // 2, 2 * K], U8, name="w1_high", tag=spent[EARLY], align_bytes=64))
+        nc.sync.dma_start(w1_w[1][:].bitcast(I32), w1_rows[:, 4:8, :].bitcast(I32))
         weave_pairs()
         make_factor(factor_upper[:, 2:4, :], two_planes(a_upper[1][:]), UPPER)
         quantize(EARLY)

@@ -1,6 +1,7 @@
 from contextlib import ExitStack
 
 import concourse.mybir as mybir
+from concourse.masks import make_identity
 
 K, T, E, C, H, N = 512, 512, 8, 128, 512, 512
 S = E * C
@@ -48,16 +49,20 @@ def tile_moe_sdb_relu2_kernel(
         offs_t = keep.tile([P, S // 16], U16, name="offs_t")
         pos1_t = keep.tile([P, T // 16], U16, name="pos1_t")
         pos2_t = keep.tile([P, T // 16], U16, name="pos2_t")
-        dy_w = keep.tile([P, T], U32, name="dy_w", tag="dy_w", align_bytes=64)
+        dy_w = keep.tile([P, T], U32, name="dy_w", align_bytes=64)
         dy_rows = keep.tile([4, 4, T], U8, name="dy_rows", align_bytes=64)
         dy_s = keep.tile([P, T], U8, name="dy_s", align_bytes=64)
         w2_raw = keep.tile([P, 2 * H], U8, name="w2_raw", align_bytes=64)
-        w2_w = keep.tile([P, 2 * H], U8, name="w2_w", tag="w2_w", align_bytes=64)
+        w2_w = keep.tile([P, 2 * H], U8, name="w2_w", align_bytes=64)
         w2_s_raw = keep.tile([P, H], U8, name="w2_s_raw", align_bytes=64)
-        w2_s = keep.tile([P, H], U8, name="w2_s", tag="w2_s", align_bytes=64)
+        w2_s = keep.tile([P, H], U8, name="w2_s", align_bytes=64)
         w1_w = [keep.tile([P, E // 2, 2 * K], U8, name="w1_low", align_bytes=64)]
         w1_s = keep.tile([P, E, K], U8, name="w1_s", align_bytes=64)
-        gate_t = keep.tile([P, S - OWN[1]], F32, name="gate_t")
+        gate_early = keep.tile([P, EARLY[1]], F32, name="gate_early")
+        gate_rows = keep.tile([P, C], F32, name="gate_rows", tag="gate_rows", align_bytes=64)
+        gate_cols = keep.tile([P, HALF // C], F32, name="gate_cols", tag="gate_cols", align_bytes=64)
+        identity = keep.tile([P, P], F32, name="identity", tag="identity", align_bytes=64)
+        gate_upper = bank(6)
         a_early = [keep.tile([P, 2, EARLY[1]], F32, name="a_early_%d" % u) for u in range(2)]
         a_upper = [keep.tile([P, 2 * HALF], F32, name="a_upper_%d" % u, align_bytes=64) for u in range(2)]
         a_own = [keep.tile([P, 2, OWN[1]], F32, name="a_own_%d" % u) for u in range(2)]
@@ -73,12 +78,16 @@ def tile_moe_sdb_relu2_kernel(
         nc.vector.memset(dy_s[:].bitcast(I32), 0)
         nc.vector.memset(w1_s[:].rearrange("p e k -> p (e k)").bitcast(I32), 0)
 
+        make_identity(nc, identity[:])
+
         a_planes = a.rearrange("(p t) s -> p t s", t=4)
 
         def gate_of(group):
             if group == OWN:
-                return factor_upper[:, 1, 0 : OWN[1]]
-            return gate_t[:, group[0] - OWN[1] : group[0] - OWN[1] + group[1]]
+                return factor_upper[:, 0, 0 : OWN[1]]
+            if group == EARLY:
+                return gate_early[:]
+            return gate_upper[:]
 
         def load_gate(group):
             nc.sync.dma_start(gate_of(group), gate[:, slots(group)])
@@ -99,9 +108,10 @@ def tile_moe_sdb_relu2_kernel(
         nc.sync.dma_start(a_early[1][:], a_planes[:, 2:4, slots(EARLY)])
         nc.sync.dma_start(offs_t[:], offs)
         load_gate(OWN)
+        nc.sync.dma_start(gate_rows[:], gate[0 : P // E, :].rearrange("r (e u) -> (r e) u", u=C))
         nc.sync.dma_start(a_own[0][:], a_planes[:, 0:2, slots(OWN)])
-        load_gate(UPPER)
-        load_upper(0)
+        for t in range(2):
+            nc.sync.dma_start(a_upper[0][:, t * HALF : (t + 1) * HALF], a_planes[:, t, slots(UPPER)])
         nc.sync.dma_start(a_own[1][:], a_planes[:, 2:4, slots(OWN)])
         load_upper(1)
         w1_rows = w1t_words.rearrange("e o p n -> p (e o) n")
@@ -127,8 +137,8 @@ def tile_moe_sdb_relu2_kernel(
         )
 
         def make_factor(factor, a_group, group):
-            gate_cols = gate_of(group).unsqueeze(1).broadcast_to(list(factor.shape))
-            nc.vector.scalar_tensor_tensor(factor, a_group, 0.0, gate_cols, MAX, MULT)
+            weights = gate_of(group).unsqueeze(1).broadcast_to(list(factor.shape))
+            nc.vector.scalar_tensor_tensor(factor, a_group, 0.0, weights, MAX, MULT)
 
         dc = [keep.tile([P, T], F32, name="dc_%d" % t) for t in range(4)]
 
@@ -152,13 +162,19 @@ def tile_moe_sdb_relu2_kernel(
         for t in range(1, 4):
             first_product(t, 0, T, t)
 
+        turned = bank(5)
+        nc.tensor.transpose(turned[:, 0:P], gate_rows[:], identity[:])
+        nc.scalar.activation(gate_cols[:], turned[:, HALF // C : E], COPY)
+        for e in range(HALF // C):
+            nc.tensor.transpose(gate_upper[:, e * C : (e + 1) * C], gate_cols[:, e : e + 1].to_broadcast([P, P]), identity[:])
+
         def window(t, group):
             return dc[t][:].indirect(offs_t[:, group[0] // 16 : (group[0] + group[1]) // 16])
 
         picked = {}
         picked_flat = {}
 
-        spent = {EARLY: "dy_w", LONG: "w2_w", LAST: "w2_s", OWN: "picked_own"}
+        spent = {EARLY: "gate_rows", LONG: "identity", LAST: "gate_cols", OWN: "picked_own"}
 
         def gather(group):
             picked_flat[group] = keep.tile(
@@ -178,7 +194,7 @@ def tile_moe_sdb_relu2_kernel(
         pairs = pairs_flat[:, 0 : 2 * OWN[1]].bitcast(BF16).rearrange("p (u s d) -> p u s d", u=2, d=2)
         da_own = keep.tile([P, 4 * OWN[1]], BF16, name="da_own", align_bytes=64)
         da = {
-            EARLY: a_upper[0][:, 0 : 2 * EARLY[1]].bitcast(BF16),
+            EARLY: a_upper[0][:, HALF : HALF + 2 * EARLY[1]].bitcast(BF16),
             OWN: da_own[:],
             LONG: pairs_flat[:].bitcast(BF16),
             LAST: da_own[:, 0 : 4 * LAST[1]],
@@ -245,7 +261,8 @@ def tile_moe_sdb_relu2_kernel(
             return factor_upper[:, :, group[0] - HALF : group[0] - HALF + group[1]]
 
         make_pairs(0)
-        make_factor(factor_upper[:, 0:2, :], two_planes(a_upper[0][:]), UPPER)
+        for t in range(2):
+            make_factor(factor_upper[:, t : t + 1, :], two_planes(a_upper[0][:])[:, t : t + 1, :], UPPER)
         make_pairs(1)
         make_da(EARLY, factor_early)
         w1_w.append(keep.tile([P, E // 2, 2 * K], U8, name="w1_high", tag=spent[EARLY], align_bytes=64))

from contextlib import ExitStack

import concourse.mybir as mybir
from concourse.masks import make_identity

K, T, E, C, H, N = 512, 512, 8, 128, 512, 512
S = E * C
P = 128
FLOPS = 2 * N * H * T + 2 * H * K * S

F32 = mybir.dt.float32
BF16 = mybir.dt.bfloat16
I32 = mybir.dt.int32
U32 = mybir.dt.uint32
U16 = mybir.dt.uint16
U8 = mybir.dt.uint8
FP8X4 = mybir.dt.float8_e4m3fn_x4
FP4X4 = mybir.dt.float4_e2m1fn_x4
MULT = mybir.AluOpType.mult
ADD = mybir.AluOpType.add
MAX = mybir.AluOpType.max
COPY = mybir.ActivationFunctionType.Copy

OWN = (0, 2 * C)
EARLY = (2 * C, 2 * C)
LAST = (4 * C, C)
LONG = (5 * C, 3 * C)
HALF = S // 2
UPPER = (HALF, HALF)


def tile_moe_sdb_relu2_kernel(
    tc, dy_words, dy_scales, w2t_words, w2t_scales, w1t_words, w1t_scales, a, gate, offs, pos1, pos2, out
):
    nc = tc.nc
    with ExitStack() as ctx:
        keep = ctx.enter_context(tc.tile_pool(name="keep", bufs=1))
        psum = ctx.enter_context(tc.psum_pool(name="psum", bufs=1))

        def bank(number):
            return psum.tile([P, T], F32, name="bank_%d" % number, tag="bank_%d" % number)

        def planes(flat):
            return flat.rearrange("p (t s) -> p t s", t=4)

        def slots(group):
            return slice(group[0], group[0] + group[1])

        offs_t = keep.tile([P, S // 16], U16, name="offs_t")
        pos1_t = keep.tile([P, T // 16], U16, name="pos1_t")
        pos2_t = keep.tile([P, T // 16], U16, name="pos2_t")
        dy_w = keep.tile([P, T], U32, name="dy_w", align_bytes=64)
        dy_rows = keep.tile([4, 4, T], U8, name="dy_rows", align_bytes=64)
        dy_s = keep.tile([P, T], U8, name="dy_s", align_bytes=64)
        w2_raw = keep.tile([P, 2 * H], U8, name="w2_raw", align_bytes=64)
        w2_w = keep.tile([P, 2 * H], U8, name="w2_w", align_bytes=64)
        w2_s_raw = keep.tile([P, H], U8, name="w2_s_raw", align_bytes=64)
        w2_s = keep.tile([P, H], U8, name="w2_s", align_bytes=64)
        w1_w = [keep.tile([P, E // 2, 2 * K], U8, name="w1_low", align_bytes=64)]
        w1_s = keep.tile([P, E, K], U8, name="w1_s", align_bytes=64)
        gate_early = keep.tile([P, EARLY[1]], F32, name="gate_early")
        gate_rows = keep.tile([P, C], F32, name="gate_rows", tag="gate_rows", align_bytes=64)
        gate_cols = keep.tile([P, HALF // C], F32, name="gate_cols", tag="gate_cols", align_bytes=64)
        identity = keep.tile([P, P], F32, name="identity", tag="identity", align_bytes=64)
        gate_upper = bank(6)
        a_early = [keep.tile([P, 2, EARLY[1]], F32, name="a_early_%d" % u) for u in range(2)]
        a_upper = [keep.tile([P, 2 * HALF], F32, name="a_upper_%d" % u, align_bytes=64) for u in range(2)]
        a_own = [keep.tile([P, 2, OWN[1]], F32, name="a_own_%d" % u) for u in range(2)]
        factor_upper = keep.tile([P, 4, HALF], F32, name="factor_upper")
        factor_early = planes(factor_upper[:, 2:4, :].rearrange("p t s -> p (t s)"))

        warm_in = keep.tile([P, 1], F32, name="warm_in")
        warm_out = keep.tile([P, 1], F32, name="warm_out")
        nc.gpsimd.memset(warm_in[:], 0.0)
        nc.scalar.activation(warm_out[:], warm_in[:], COPY)

        nc.vector.memset(w2_s_raw[:].bitcast(I32), 0)
        nc.vector.memset(dy_s[:].bitcast(I32), 0)
        nc.vector.memset(w1_s[:].rearrange("p e k -> p (e k)").bitcast(I32), 0)

        make_identity(nc, identity[:])

        a_planes = a.rearrange("(p t) s -> p t s", t=4)

        def gate_of(group):
            if group == OWN:
                return factor_upper[:, 0, 0 : OWN[1]]
            if group == EARLY:
                return gate_early[:]
            return gate_upper[:]

        def load_gate(group):
            nc.sync.dma_start(gate_of(group), gate[:, slots(group)])

        def two_planes(flat):
            return flat.rearrange("p (t s) -> p t s", t=2)

        def load_upper(u):
            nc.sync.dma_start(two_planes(a_upper[u][:]), a_planes[:, 2 * u : 2 * u + 2, slots(UPPER)])

        nc.sync.dma_start(dy_rows[:].bitcast(I32), dy_scales[0].rearrange("(q r) t -> r q t", r=4).bitcast(I32))
        nc.sync.dma_start(w2_raw[:].bitcast(I32), w2t_words[0].bitcast(I32))
        nc.sync.dma_start(dy_w[:].bitcast(I32), dy_words[0].rearrange("p t d -> p (t d)").bitcast(I32))
        for r in range(4):
            nc.sync.dma_start(w2_s_raw[r:P:32, :].bitcast(I32), w2t_scales[0, r:16:4, :].bitcast(I32))
        nc.sync.dma_start(a_early[0][:], a_planes[:, 0:2, slots(EARLY)])
        load_gate(EARLY)
        nc.sync.dma_start(a_early[1][:], a_planes[:, 2:4, slots(EARLY)])
        nc.sync.dma_start(offs_t[:], offs)
        load_gate(OWN)
        nc.sync.dma_start(gate_rows[:], gate[0 : P // E, :].rearrange("r (e u) -> (r e) u", u=C))
        nc.sync.dma_start(a_own[0][:], a_planes[:, 0:2, slots(OWN)])
        for t in range(2):
            nc.sync.dma_start(a_upper[0][:, t * HALF : (t + 1) * HALF], a_planes[:, t, slots(UPPER)])
        nc.sync.dma_start(a_own[1][:], a_planes[:, 2:4, slots(OWN)])
        load_upper(1)
        w1_rows = w1t_words.rearrange("e o p n -> p (e o) n")
        nc.sync.dma_start(w1_w[0][:].bitcast(I32), w1_rows[:, 0:4, :].bitcast(I32))
        for r in range(4):
            nc.sync.dma_start(
                w1_s[r:P:32, :, :].bitcast(I32),
                w1t_scales[:, 0, r:16:4, :].rearrange("e q k -> q e k").bitcast(I32),
            )
        nc.sync.dma_start(pos1_t[:], pos1)
        nc.sync.dma_start(pos2_t[:], pos2)

        nc.scalar.copy(dy_s[0:4, :].bitcast(U32), dy_rows[:, 0, :].bitcast(U32))
        for q in range(1, 4):
            nc.vector.tensor_copy(dy_s[32 * q : 32 * q + 4, :].bitcast(I32), dy_rows[:, q, :].bitcast(I32))
        nc.scalar.copy(
            w2_w[:].bitcast(U16).rearrange("p (t m) -> p t m", t=4),
            w2_raw[:].bitcast(U16).rearrange("p (m t) -> p t m", t=4),
        )
        nc.vector.tensor_copy(
            w2_s[:].rearrange("p (t m) -> p t m", t=4),
            w2_s_raw[:].rearrange("p (m t) -> p t m", t=4),
        )

        def make_factor(factor, a_group, group):
            weights = gate_of(group).unsqueeze(1).broadcast_to(list(factor.shape))
            nc.vector.scalar_tensor_tensor(factor, a_group, 0.0, weights, MAX, MULT)

        dc = [keep.tile([P, T], F32, name="dc_%d" % t) for t in range(4)]

        def first_product(t, n0, w, number):
            acc = bank(number)
            nc.tensor.matmul_mx(
                out=acc[:, 0:w],
                lhsT=w2_w[:, 2 * P * t : 2 * P * (t + 1)].bitcast(FP4X4),
                lhsT_scale=w2_s[:, P * t : P * (t + 1)],
                rhs=dy_w[:, n0 : n0 + w].bitcast(FP8X4),
                rhs_scale=dy_s[:, n0 : n0 + w],
                start=True,
                stop=True,
            )
            nc.scalar.activation(dc[t][:, n0 : n0 + w], acc[:, 0:w], COPY, scale=2.0)

        for u in range(2):
            make_factor(factor_early[:, 2 * u : 2 * u + 2, :], a_early[u][:], EARLY)
        first_product(0, 0, T // 2, 0)
        first_product(0, T // 2, T // 2, 4)
        for t in range(1, 4):
            first_product(t, 0, T, t)

        turned = bank(5)
        nc.tensor.transpose(turned[:, 0:P], gate_rows[:], identity[:])
        nc.scalar.activation(gate_cols[:], turned[:, HALF // C : E], COPY)
        for e in range(HALF // C):
            nc.tensor.transpose(gate_upper[:, e * C : (e + 1) * C], gate_cols[:, e : e + 1].to_broadcast([P, P]), identity[:])

        def window(t, group):
            return dc[t][:].indirect(offs_t[:, group[0] // 16 : (group[0] + group[1]) // 16])

        picked = {}
        picked_flat = {}

        spent = {EARLY: "gate_rows", LONG: "identity", LAST: "gate_cols", OWN: "picked_own"}

        def gather(group):
            picked_flat[group] = keep.tile(
                [P, 4 * group[1]], F32, name="picked_%d" % group[0], tag=spent[group], align_bytes=64
            )
            picked[group] = planes(picked_flat[group][:])
            for t in range(4):
                if group == OWN:
                    nc.vector.tensor_tensor(picked[group][:, t, :], window(t, group), gate_of(group), MULT)
                else:
                    nc.scalar.activation(picked[group][:, t, :], window(t, group), COPY)

        for group in (EARLY, OWN, LONG, LAST):
            gather(group)

        pairs_flat = keep.tile([P, 2 * LONG[1]], F32, name="pairs", tag="pairs", align_bytes=64)
        pairs = pairs_flat[:, 0 : 2 * OWN[1]].bitcast(BF16).rearrange("p (u s d) -> p u s d", u=2, d=2)
        da_own = keep.tile([P, 4 * OWN[1]], BF16, name="da_own", align_bytes=64)
        da = {
            EARLY: a_upper[0][:, HALF : HALF + 2 * EARLY[1]].bitcast(BF16),
            OWN: da_own[:],
            LONG: pairs_flat[:].bitcast(BF16),
            LAST: da_own[:, 0 : 4 * LAST[1]],
        }
        codes = keep.tile([P, S], U32, name="codes", align_bytes=64)
        scales = keep.tile([P, S], U8, name="scales", align_bytes=64)

        def make_da(group, factor):
            nc.vector.tensor_tensor(
                da[group].rearrange("p (c i t) -> p c t i", i=2, t=4),
                picked[group].rearrange("p t (c i) -> p c t i", i=2),
                factor.rearrange("p t (c i) -> p c t i", i=2),
                MULT,
            )

        def make_pairs(u):
            nc.vector.scalar_tensor_tensor(
                pairs[:, u, :, :],
                a_own[u][:].rearrange("p d s -> p s d"),
                0.0,
                picked[OWN][:, 2 * u : 2 * u + 2, :].rearrange("p d s -> p s d"),
                MAX,
                MULT,
            )

        def weave_pairs():
            nc.vector.tensor_copy(
                da[OWN].bitcast(F32).rearrange("p (s u) -> p s u", u=2),
                pairs.rearrange("p u s d -> p u (s d)").bitcast(F32).rearrange("p u s -> p s u"),
            )

        def quantize(group):
            nc.vector.quantize_mx(
                out=codes[:, slots(group)].bitcast(FP8X4), scales=scales[:, slots(group)], in_=da[group]
            )

        dx = [keep.tile([P, S], F32, name="dx_%d" % b) for b in range(3)]
        accs = {}

        def second_product(group, b):
            e0 = group[0] // C
            key = (e0 // 4, b)
            if key not in accs:
                accs[key] = bank(4 * (e0 // 4) + b)
            for e in range(e0, e0 + group[1] // C):
                nc.tensor.matmul_mx(
                    out=accs[key][:, (e % 4) * C : (e % 4 + 1) * C],
                    lhsT=w1_w[e // 4][:, e % 4, 2 * P * b : 2 * P * (b + 1)].bitcast(FP4X4),
                    lhsT_scale=w1_s[:, e, P * b : P * (b + 1)],
                    rhs=codes[:, e * C : (e + 1) * C].bitcast(FP8X4),
                    rhs_scale=scales[:, e * C : (e + 1) * C],
                    start=True,
                    stop=True,
                )

        def empty(h, b, on_scalar):
            dst = dx[b][:, h * HALF : (h + 1) * HALF]
            if on_scalar:
                nc.scalar.activation(dst, accs[h, b][:], COPY)
            else:
                nc.vector.tensor_copy(dst, accs[h, b][:])

        def upper_factor(group):
            return factor_upper[:, :, group[0] - HALF : group[0] - HALF + group[1]]

        make_pairs(0)
        for t in range(2):
            make_factor(factor_upper[:, t : t + 1, :], two_planes(a_upper[0][:])[:, t : t + 1, :], UPPER)
        make_pairs(1)
        make_da(EARLY, factor_early)
        w1_w.append(keep.tile([P, E // 2, 2 * K], U8, name="w1_high", tag=spent[EARLY], align_bytes=64))
        nc.sync.dma_start(w1_w[1][:].bitcast(I32), w1_rows[:, 4:8, :].bitcast(I32))
        weave_pairs()
        make_factor(factor_upper[:, 2:4, :], two_planes(a_upper[1][:]), UPPER)
        quantize(EARLY)
        quantize(OWN)
        for b in range(4):
            second_product(EARLY, b)
            second_product(OWN, b)
            if b < 3:
                empty(0, b, True)
        make_da(LONG, upper_factor(LONG))
        make_da(LAST, upper_factor(LAST))
        quantize(LONG)
        quantize(LAST)
        dx.append(keep.tile([P, S], F32, name="dx_3", tag="pairs", align_bytes=64))
        empty(0, 3, False)
        second_product(LONG, 0)
        for b in range(4):
            second_product(LAST, b)
            if b:
                second_product(LONG, b)

        first = [keep.tile([P, T], F32, name="first_%d" % b) for b in range(4)]
        total = [keep.tile([P, T], F32, name="total_%d" % b) for b in range(4)]

        def fetch(dst, b, pos_t, t0, t1):
            nc.scalar.activation(dst, dx[b][:].indirect(pos_t[:, t0 // 16 : t1 // 16]), COPY)

        def add_second(b, t0, t1):
            nc.vector.tensor_tensor(
                total[b][:, t0:t1], dx[b][:].indirect(pos2_t[:, t0 // 16 : t1 // 16]), first[b][:, t0:t1], ADD
            )

        def store(b, t0, t1):
            nc.sync.dma_start(out[b * P : (b + 1) * P, t0:t1], total[b][:, t0:t1])

        for b in range(4):
            empty(1, b, b == 0)
        for b in range(3):
            fetch(first[b][:], b, pos1_t, 0, T)
            add_second(b, 0, T)
            store(b, 0, T)
        cut = 256
        second = keep.tile([P, T - cut], F32, name="second")
        fetch(first[3][:], 3, pos1_t, 0, T)
        fetch(second[:], 3, pos2_t, cut, T)
        add_second(3, 0, cut)
        store(3, 0, cut)
        nc.vector.tensor_tensor(total[3][:, cut:T], second[:], first[3][:, cut:T], ADD)
        store(3, cut, T)
